import numpy as np
import ml_dtypes


def mxq(x, axis, fmt="e4m3"):
    dtype, down = {"e4m3": (ml_dtypes.float8_e4m3fn, 7), "e5m2": (ml_dtypes.float8_e5m2, 14)}[fmt]
    v = np.moveaxis(np.asarray(x, np.float32).astype(ml_dtypes.bfloat16).astype(np.float64), axis, -1)
    blocks = v.reshape(v.shape[:-1] + (-1, 32))
    amax = np.abs(blocks).max(-1, keepdims=True)
    byte = np.maximum(np.where(amax > 0, np.frexp(amax)[1] - 1 + 127, 0) - down, 1)
    scale = np.exp2(byte - 127.0)
    codes = (blocks / scale).astype(np.float32).astype(dtype).astype(np.float64)
    return np.moveaxis((codes * scale).reshape(v.shape), -1, axis)


WIDE = False


def mx_kscale(k):
    if not WIDE:
        return np.ones(k)
    levels = np.array([10, -10, 5, -5, 0])
    if k % 512:
        return np.exp2(np.random.permutation(np.resize(levels, k // 32))).repeat(32)
    a = np.empty((k // 512, 16))
    for p in range(k // 512):
        a[p, :8] = np.random.permutation(np.resize(levels, 8))
        for g in range(8):
            far = levels[np.abs(levels - a[p, g]) >= 10]
            a[p, g + 8] = far[np.random.randint(len(far))]
    return np.exp2(a.ravel()).repeat(32)


def f64(x):
    return np.asarray(x).astype(np.float64)


def striped(idx):
    return np.tile(idx.reshape(-1, 16).T, (8, 1)).astype(np.uint16)


def unstriped(offs):
    return offs[:16].T.reshape(-1).astype(np.int64)


def silu(v):
    return v / (1.0 + np.exp(-np.maximum(v, -700.0)))


K, T, D, S, V, H, N = 1536, 1024, 4, 512, 256, 512, 512


def setup_inputs():
    n = np.random.standard_normal
    s = mx_kscale(K)[:, None]
    u = mx_kscale(H)
    return {
        "xT": (n((K, T)) * s).astype(np.float32),
        "w1": (n((K, H)) / np.sqrt(K) / s * u).astype(np.float32),
        "w2": (n((H, N)) / np.sqrt(H) / u[:, None]).astype(np.float32),
        "gate": np.tile(np.random.uniform(0.2, 1.0, (D, 1, V)) / np.sqrt(D), (1, N, 1)).astype(np.float32),
        "offs": striped(np.random.permutation(T)[:S]),
        "pos1": striped(np.random.permutation(S)[:V]),
        "pos2": striped(np.random.permutation(S)[:V]),
        "pos3": striped(np.random.permutation(S)[:V]),
        "pos4": striped(np.random.permutation(S)[:V]),
    }


def reference(xT, w1, w2, gate, offs, pos1, pos2, pos3, pos4):
    idx = unstriped(offs)
    xq = mxq(f64(xT)[:, idx], 0, "e4m3")
    h = silu(mxq(f64(w1), 0, "e4m3").T @ xq)
    y = mxq(f64(w2), 0, "e4m3").T @ mxq(h, 0, "e4m3")
    return sum(f64(gate[d]) * y[:, unstriped(p)] for d, p in enumerate((pos1, pos2, pos3, pos4)))

@@ -1,0 +1,236 @@
+from contextlib import ExitStack
+
+import concourse.mybir as mybir
+
+K, T, S, H, N, V, D = 1536, 1024, 512, 512, 512, 256, 4
+FLOPS = 2 * K * H * S + 2 * H * N * S
+
+F32 = mybir.dt.float32
+BF16 = mybir.dt.bfloat16
+U32 = mybir.dt.uint32
+U16 = mybir.dt.uint16
+U8 = mybir.dt.uint8
+FP8X4 = mybir.dt.float8_e4m3fn_x4
+COPY = mybir.ActivationFunctionType.Copy
+SILU = mybir.ActivationFunctionType.Silu
+MULT = mybir.AluOpType.mult
+ADD = mybir.AluOpType.add
+
+P = 128
+G = K // 512
+M_TILES = N // P
+A = 256
+
+
+def tile_picked_sub_mlp_silu_sub_e_kernel(tc, xT, w1, w2, gate, offs, pos1, pos2, pos3, pos4, out):
+    nc = tc.nc
+    with ExitStack() as ctx:
+        keep = ctx.enter_context(tc.tile_pool(name="keep", bufs=1))
+        psum = ctx.enter_context(tc.psum_pool(name="psum", bufs=1))
+
+        def sb(name, shape, dtype):
+            return keep.tile(shape, dtype, name=name, align_bytes=64)
+
+        offs_sb = sb("offs_sb", [P, S // 16], U16)
+        pos_sb = [sb(f"pos_sb{d}", [P, V // 16], U16) for d in range(D)]
+        pieces = [(0, 256, "s"), (512, 768, "v"), (256, 512, "s"), (768, 1024, "v")]
+        x_raw = [sb(f"x_raw{g}", [P, 4, T], F32) for g in range(G)]
+        x_grp = [[sb(f"x_grp{g}_{t0}", [P, t1 - t0, 4], BF16) for t0, t1, e in pieces] for g in range(G)]
+        x_words = [sb(f"x_words{g}", [P, T], U32) for g in range(G)]
+        x_bytes = sb("x_bytes", [P, T], U8)
+        p_words = [sb(f"p_words{g}", [P, S], U32) for g in range(G)]
+        p_bytes = sb("p_bytes", [P, S], U8)
+        w1_raw = [sb(f"w1_raw{g}", [P, 4, H], F32) for g in range(G)]
+        w1_grp = [sb(f"w1_grp{g}", [P, 4 * H], BF16) for g in range(G)]
+        w1_words = [sb(f"w1_words{g}", [P, H], U32) for g in range(G)]
+        w1_bytes = [sb(f"w1_bytes{g}", [P, H], U8) for g in range(G)]
+        w2_raw = sb("w2_raw", [P, 4, N], F32)
+        w2_grp = sb("w2_grp", [P, N, 4], BF16)
+        w2_words = sb("w2_words", [P, N], U32)
+        w2_bytes = sb("w2_bytes", [P, N], U8)
+        h_flat = sb("h_flat", [P, 4, A], BF16)
+        h_grp_a = sb("h_grp_a", [P, A, 4], BF16)
+        h_grp_b = [sb(f"h_grp_b{s}", [P, P, 4], BF16) for s in range(2)]
+        h_words = sb("h_words", [P, S], U32)
+        h_bytes = sb("h_bytes", [P, S], U8)
+        gates = [sb(f"gates{m}", [P, D, V], F32) for m in range(M_TILES)]
+        y_sb = [sb(f"y_sb{m}", [P, S], F32) for m in range(M_TILES)]
+        terms = [sb(f"terms{m}", [P, D, V], F32) for m in range(M_TILES)]
+        pairs = [sb(f"pairs{m}", [P, 2, V], F32) for m in range(M_TILES)]
+        sums = [sb(f"sums{m}", [P, V], F32) for m in range(M_TILES)]
+        warm = sb("warm", [P, 1], F32)
+
+        def load_x(g):
+            nc.sync.dma_start(out=x_raw[g][:], in_=xT[512 * g : 512 * (g + 1), :].rearrange("(p j) t -> p j t", j=4))
+
+        load_x(0)
+        nc.sync.dma_start(offs_sb[:], offs)
+        load_x(1)
+        load_x(2)
+        for g in range(G):
+            nc.sync.dma_start(out=w1_raw[g][:], in_=w1[512 * g : 512 * (g + 1), :].rearrange("(p j) c -> p j c", j=4))
+        nc.sync.dma_start(out=w2_raw[:], in_=w2.rearrange("(p j) c -> p j c", j=4))
+        for d, pos in enumerate((pos1, pos2, pos3, pos4)):
+            nc.sync.dma_start(pos_sb[d][:], pos)
+        for m in range(M_TILES):
+            for d0, d1 in ((0, 2), (2, 4)) if m == 0 else ((0, 4),):
+                rows = gate[d0:d1, P * m : P * (m + 1), :].rearrange("d p v -> p d v")
+                nc.sync.dma_start(out=gates[m][:, d0:d1, :], in_=rows)
+
+        nc.gpsimd.memset(x_bytes[:], 0)
+        nc.vector.memset(warm[:], 0.0)
+        nc.scalar.activation(warm[:], warm[:], SILU)
+
+        def cast_x(g, i):
+            t0, t1, engine = pieces[i]
+            src = x_raw[g][:, :, t0:t1].rearrange("p j (c i) -> p c j i", i=4)
+            dst = x_grp[g][i][:].rearrange("p (c i) j -> p c j i", i=4)
+            if engine == "v":
+                nc.vector.tensor_copy(dst, src)
+            else:
+                nc.scalar.activation(dst, src, COPY)
+
+        def quant_x(g, i):
+            t0, t1, engine = pieces[i]
+            nc.vector.quantize_mx(
+                out=x_words[g][:, t0:t1].bitcast(FP8X4),
+                scales=x_bytes[4 * g : P, t0:t1],
+                in_=x_grp[g][i][:].rearrange("p c j -> p (c j)"),
+            )
+
+        def cast_w1(g, engine, m0, m1, ts=slice(0, 4)):
+            src = w1_raw[g][:].rearrange("p j (m t) -> p m j t", t=4)[:, m0:m1, :, ts]
+            dst = w1_grp[g][:].rearrange("p (t m j) -> p m j t", t=4, j=4)[:, m0:m1, :, ts]
+            if engine == "v":
+                nc.vector.tensor_copy(dst, src)
+            else:
+                nc.scalar.activation(dst, src, COPY)
+
+        def quant_w1(g, t0, t1):
+            nc.vector.quantize_mx(
+                out=w1_words[g][:, P * t0 : P * t1].bitcast(FP8X4),
+                scales=w1_bytes[g][:, P * t0 : P * t1],
+                in_=w1_grp[g][:, 512 * t0 : 512 * t1],
+            )
+
+        for g in range(G):
+            for half in ((0, 1), (2, 3)):
+                for i in half:
+                    cast_x(g, i)
+                for i in half:
+                    quant_x(g, i)
+            nc.vector.tensor_copy(p_words[g][:], x_words[g][:].indirect(offs_sb[:]))
+        nc.vector.tensor_copy(p_bytes[:], x_bytes[:].indirect(offs_sb[:]))
+
+        acc_a = [psum.tile([P, A], F32, name=f"acc_a{t}") for t in range(4)]
+        acc_b = [psum.tile([P, 4, P], F32, name=f"acc_b{s}") for s in range(2)]
+
+        def layer1(dst, t, c0, c1, g):
+            nc.tensor.matmul_mx(
+                out=dst,
+                lhsT=w1_words[g][:, P * t : P * (t + 1)].bitcast(FP8X4),
+                lhsT_scale=w1_bytes[g][:, P * t : P * (t + 1)],
+                rhs=p_words[g][:, c0:c1].bitcast(FP8X4),
+                rhs_scale=p_bytes[4 * g : P, c0:c1],
+                start=(g == 0),
+                stop=(g == G - 1),
+            )
+
+        def layer1_b(s, t, g):
+            layer1(acc_b[s][:, t, :], t, A + P * s, A + P * (s + 1), g)
+
+        for g in range(G):
+            split = (P, 64, 44)[g]
+            cast_w1(g, "s", 0, split)
+            if split < P:
+                cast_w1(g, "v", split, P, slice(0, 2))
+                cast_w1(g, "v", split, P, slice(2, 4))
+            if g < 2:
+                quant_w1(g, 0, 4)
+            else:
+                quant_w1(g, 0, 1)
+                quant_w1(g, 1, 2)
+                quant_w1(g, 2, 4)
+            for t in range(4):
+                layer1(acc_a[t][:], t, 0, A, g)
+            for s in range(2):
+                layer1_b(s, 0, g)
+        for s in range(2):
+            for t in range(1, 4):
+                for g in range(G):
+                    layer1_b(s, t, g)
+
+        nc.vector.tensor_copy(
+            w2_grp[:].rearrange("p (c i) j -> p c j i", i=4), w2_raw[:].rearrange("p j (c i) -> p c j i", i=4)
+        )
+        nc.vector.quantize_mx(
+            out=w2_words[:].bitcast(FP8X4), scales=w2_bytes[:], in_=w2_grp[:].rearrange("p c j -> p (c j)")
+        )
+
+        for t in range(4):
+            nc.scalar.activation(h_flat[:, t, :], acc_a[t][:], SILU)
+        for s in range(2):
+            nc.scalar.activation(h_grp_b[s][:], acc_b[s][:].rearrange("p t n -> p n t"), SILU)
+
+        nc.vector.tensor_copy(
+            h_grp_a[:].rearrange("p (c i) t -> p c t i", i=4), h_flat[:].rearrange("p t (c i) -> p c t i", i=4)
+        )
+
+        def quant_h(grp, c0, c1):
+            nc.vector.quantize_mx(
+                out=h_words[:, c0:c1].bitcast(FP8X4),
+                scales=h_bytes[:, c0:c1],
+                in_=grp[:].rearrange("p n t -> p (n t)"),
+            )
+
+        quant_h(h_grp_a, 0, A)
+        for s in range(2):
+            quant_h(h_grp_b[s], A + P * s, A + P * (s + 1))
+
+        tags = ("acc_y0", "acc_y1", "acc_a0", "acc_a1")
+        acc_y = [psum.tile([P, S], F32, name=f"acc_y{m}", tag=tags[m]) for m in range(M_TILES)]
+
+        def layer2(m):
+            for c0, c1 in ((0, A), (A, A + P), (A + P, S)):
+                nc.tensor.matmul_mx(
+                    out=acc_y[m][:, c0:c1],
+                    lhsT=w2_words[:, P * m : P * (m + 1)].bitcast(FP8X4),
+                    lhsT_scale=w2_bytes[:, P * m : P * (m + 1)],
+                    rhs=h_words[:, c0:c1].bitcast(FP8X4),
+                    rhs_scale=h_bytes[:, c0:c1],
+                    start=True,
+                    stop=True,
+                )
+
+        layer2(0)
+        nc.vector.tensor_copy(y_sb[0][:, : A + P], acc_y[0][:, : A + P])
+        nc.scalar.activation(y_sb[0][:, A + P :], acc_y[0][:, A + P :], COPY)
+        for m in range(1, M_TILES):
+            layer2(m)
+            nc.scalar.activation(y_sb[m][:], acc_y[m][:], COPY)
+
+        def fetch(m, d):
+            nc.vector.tensor_tensor(terms[m][:, d, :], y_sb[m][:].indirect(pos_sb[d][:]), gates[m][:, d, :], MULT)
+
+        def add(o, a, b):
+            nc.vector.tensor_tensor(o, a, b, ADD)
+
+        def store(m):
+            nc.sync.dma_start(out=out[P * m : P * (m + 1), :], in_=sums[m][:])
+
+        for m in range(M_TILES):
+            fetch(m, 0)
+            if m > 0:
+                add(pairs[m - 1][:], terms[m - 1][:, 0:2, :], terms[m - 1][:, 2:4, :])
+            fetch(m, 1)
+            if m > 0:
+                add(sums[m - 1][:], pairs[m - 1][:, 0, :], pairs[m - 1][:, 1, :])
+                store(m - 1)
+            fetch(m, 2)
+            if m == M_TILES - 1:
+                add(pairs[m][:, 0, :], terms[m][:, 0, :], terms[m][:, 1, :])
+            fetch(m, 3)
+        m = M_TILES - 1
+        add(pairs[m][:, 1, :], pairs[m][:, 0, :], terms[m][:, 2, :])
+        add(sums[m][:], pairs[m][:, 1, :], terms[m][:, 3, :])
+        store(m)

@@ -1,6 +1,7 @@
 from contextlib import ExitStack
 
 import concourse.mybir as mybir
+from concourse.masks import make_identity
 
 K, T, S, H, N, V, D = 1536, 1024, 512, 512, 512, 256, 4
 FLOPS = 2 * K * H * S + 2 * H * N * S
@@ -53,10 +54,11 @@ def tile_picked_sub_mlp_silu_sub_e_kernel(tc, xT, w1, w2, gate, offs, pos1, pos2
         h_grp_b = [sb(f"h_grp_b{s}", [P, P, 4], BF16) for s in range(2)]
         h_words = sb("h_words", [P, S], U32)
         h_bytes = sb("h_bytes", [P, S], U8)
-        gates = [sb(f"gates{m}", [P, D, V], F32) for m in range(M_TILES)]
+        gates = sb("gates", [P, D, V], F32)
         y_sb = [sb(f"y_sb{m}", [P, S], F32) for m in range(M_TILES)]
         terms = [sb(f"terms{m}", [P, D, V], F32) for m in range(M_TILES)]
-        pairs = [sb(f"pairs{m}", [P, 2, V], F32) for m in range(M_TILES)]
+        turned = [sb(f"turned{m}", [P, V], F32) for m in range(M_TILES)]
+        ident = sb("ident", [P, P], F32)
         sums = [sb(f"sums{m}", [P, V], F32) for m in range(M_TILES)]
         warm = sb("warm", [P, 1], F32)
 
@@ -72,12 +74,10 @@ def tile_picked_sub_mlp_silu_sub_e_kernel(tc, xT, w1, w2, gate, offs, pos1, pos2
         nc.sync.dma_start(out=w2_raw[:], in_=w2.rearrange("(p j) c -> p j c", j=4))
         for d, pos in enumerate((pos1, pos2, pos3, pos4)):
             nc.sync.dma_start(pos_sb[d][:], pos)
-        for m in range(M_TILES):
-            for d0, d1 in ((0, 2), (2, 4)) if m == 0 else ((0, 4),):
-                rows = gate[d0:d1, P * m : P * (m + 1), :].rearrange("d p v -> p d v")
-                nc.sync.dma_start(out=gates[m][:, d0:d1, :], in_=rows)
+        nc.sync.dma_start(out=gates[:], in_=gate[:, 0:P, :].rearrange("d p v -> p d v"))
 
         nc.gpsimd.memset(x_bytes[:], 0)
+        make_identity(nc, ident[:])
         nc.vector.memset(warm[:], 0.0)
         nc.scalar.activation(warm[:], warm[:], SILU)
 
@@ -209,28 +209,43 @@ def tile_picked_sub_mlp_silu_sub_e_kernel(tc, xT, w1, w2, gate, offs, pos1, pos2
             layer2(m)
             nc.scalar.activation(y_sb[m][:], acc_y[m][:], COPY)
 
-        def fetch(m, d):
-            nc.vector.tensor_tensor(terms[m][:, d, :], y_sb[m][:].indirect(pos_sb[d][:]), gates[m][:, d, :], MULT)
+        sum_tags = ("acc_a2", "acc_a3", "acc_b0", "acc_b1")
+        acc_t = [psum.tile([P, V], F32, name=f"acc_t{m}", tag=sum_tags[m]) for m in range(M_TILES)]
+        acc_o = [psum.tile([P, V], F32, name=f"acc_o{m}", tag=tags[m]) for m in range(M_TILES)]
 
-        def add(o, a, b):
-            nc.vector.tensor_tensor(o, a, b, ADD)
+        def fetch(m, d):
+            nc.vector.tensor_tensor(terms[m][:, d, :], y_sb[m][:].indirect(pos_sb[d][:]), gates[:, d, :], MULT)
+
+        def turn_and_add(m, d, last):
+            for u in range(V // P):
+                nc.tensor.matmul(
+                    acc_t[m][:, P * u : P * (u + 1)],
+                    lhsT=terms[m][:, d, P * u : P * (u + 1)],
+                    rhs=ident[:],
+                    start=(d == 0 and u == 0),
+                    stop=(d == last and u == V // P - 1),
+                    is_transpose=True,
+                )
+
+        def turn_back(m):
+            nc.scalar.activation(turned[m][:], acc_t[m][:], COPY)
+            for u in range(V // P):
+                nc.tensor.transpose(acc_o[m][:, P * u : P * (u + 1)], turned[m][:, P * u : P * (u + 1)], ident[:])
 
         def store(m):
             nc.sync.dma_start(out=out[P * m : P * (m + 1), :], in_=sums[m][:])
 
         for m in range(M_TILES):
-            fetch(m, 0)
-            if m > 0:
-                add(pairs[m - 1][:], terms[m - 1][:, 0:2, :], terms[m - 1][:, 2:4, :])
-            fetch(m, 1)
-            if m > 0:
-                add(sums[m - 1][:], pairs[m - 1][:, 0, :], pairs[m - 1][:, 1, :])
-                store(m - 1)
-            fetch(m, 2)
-            if m == M_TILES - 1:
-                add(pairs[m][:, 0, :], terms[m][:, 0, :], terms[m][:, 1, :])
-            fetch(m, 3)
-        m = M_TILES - 1
-        add(pairs[m][:, 1, :], pairs[m][:, 0, :], terms[m][:, 2, :])
-        add(sums[m][:], pairs[m][:, 1, :], terms[m][:, 3, :])
-        store(m)
+            last = D - 1 if m < 2 else D - 2
+            for d in range(last + 1):
+                fetch(m, d)
+                turn_and_add(m, d, last)
+            turn_back(m)
+            if m < 2:
+                nc.scalar.activation(sums[m][:], acc_o[m][:], COPY)
+                store(m)
+        for m in (2, 3):
+            fetch(m, D - 1)
+        for m in (2, 3):
+            nc.vector.tensor_tensor(sums[m][:], acc_o[m][:], terms[m][:, D - 1, :], ADD)
+            store(m)

@@ -18,9 +18,9 @@ MULT = mybir.AluOpType.mult
 ADD = mybir.AluOpType.add
 
 P = 128
+A = 128
 G = K // 512
 M_TILES = N // P
-A = 256
 
 
 def tile_picked_sub_mlp_silu_sub_e_kernel(tc, xT, w1, w2, gate, offs, pos1, pos2, pos3, pos4, out):
@@ -29,8 +29,8 @@ def tile_picked_sub_mlp_silu_sub_e_kernel(tc, xT, w1, w2, gate, offs, pos1, pos2
         keep = ctx.enter_context(tc.tile_pool(name="keep", bufs=1))
         psum = ctx.enter_context(tc.psum_pool(name="psum", bufs=1))
 
-        def sb(name, shape, dtype):
-            return keep.tile(shape, dtype, name=name, align_bytes=64)
+        def sb(name, shape, dtype, tag=None):
+            return keep.tile(shape, dtype, name=name, tag=tag or name, align_bytes=64)
 
         offs_sb = sb("offs_sb", [P, S // 16], U16)
         pos_sb = [sb(f"pos_sb{d}", [P, V // 16], U16) for d in range(D)]
@@ -39,20 +39,18 @@ def tile_picked_sub_mlp_silu_sub_e_kernel(tc, xT, w1, w2, gate, offs, pos1, pos2
         x_grp = [[sb(f"x_grp{g}_{t0}", [P, t1 - t0, 4], BF16) for t0, t1, e in pieces] for g in range(G)]
         x_words = [sb(f"x_words{g}", [P, T], U32) for g in range(G)]
         x_bytes = sb("x_bytes", [P, T], U8)
-        p_words = [sb(f"p_words{g}", [P, S], U32) for g in range(G)]
+        p_words = [sb(f"p_words{g}", [P, S], U32) for g in range(G - 1)]
         p_bytes = sb("p_bytes", [P, S], U8)
         w1_raw = [sb(f"w1_raw{g}", [P, 4, H], F32) for g in range(G)]
         w1_grp = [sb(f"w1_grp{g}", [P, 4 * H], BF16) for g in range(G)]
         w1_words = [sb(f"w1_words{g}", [P, H], U32) for g in range(G)]
         w1_bytes = [sb(f"w1_bytes{g}", [P, H], U8) for g in range(G)]
         w2_raw = sb("w2_raw", [P, 4, N], F32)
-        w2_grp = sb("w2_grp", [P, N, 4], BF16)
+        w2_grp = [sb(f"w2_grp{e}", [P, N // 2, 4], BF16) for e in range(2)]
         w2_words = sb("w2_words", [P, N], U32)
         w2_bytes = sb("w2_bytes", [P, N], U8)
         h_flat = sb("h_flat", [P, 4, A], BF16)
-        h_grp_a = sb("h_grp_a", [P, A, 4], BF16)
-        h_grp_b = [sb(f"h_grp_b{s}", [P, P, 4], BF16) for s in range(2)]
-        h_words = sb("h_words", [P, S], U32)
+        h_grp = [sb(f"h_grp{s}", [P, P, 4], BF16) for s in range((S - A) // P)]
         h_bytes = sb("h_bytes", [P, S], U8)
         gates = sb("gates", [P, D, V], F32)
         y_sb = [sb(f"y_sb{m}", [P, S], F32) for m in range(M_TILES)]
@@ -119,28 +117,27 @@ def tile_picked_sub_mlp_silu_sub_e_kernel(tc, xT, w1, w2, gate, offs, pos1, pos2
                     cast_x(g, i)
                 for i in half:
                     quant_x(g, i)
-            nc.vector.tensor_copy(p_words[g][:], x_words[g][:].indirect(offs_sb[:]))
+            if g < G - 1:
+                nc.vector.tensor_copy(p_words[g][:], x_words[g][:].indirect(offs_sb[:]))
         nc.vector.tensor_copy(p_bytes[:], x_bytes[:].indirect(offs_sb[:]))
 
+        slices = (S - A) // P
         acc_a = [psum.tile([P, A], F32, name=f"acc_a{t}") for t in range(4)]
-        acc_b = [psum.tile([P, 4, P], F32, name=f"acc_b{s}") for s in range(2)]
+        acc_h = [psum.tile([P, 4, P], F32, name=f"acc_h{s}") for s in range(slices)]
 
-        def layer1(dst, t, c0, c1, g):
+        def layer1(dst, t, c0, c1, g, start, stop):
             nc.tensor.matmul_mx(
                 out=dst,
                 lhsT=w1_words[g][:, P * t : P * (t + 1)].bitcast(FP8X4),
                 lhsT_scale=w1_bytes[g][:, P * t : P * (t + 1)],
                 rhs=p_words[g][:, c0:c1].bitcast(FP8X4),
                 rhs_scale=p_bytes[4 * g : P, c0:c1],
-                start=(g == 0),
-                stop=(g == G - 1),
+                start=start,
+                stop=stop,
             )
 
-        def layer1_b(s, t, g):
-            layer1(acc_b[s][:, t, :], t, A + P * s, A + P * (s + 1), g)
-
         for g in range(G):
-            split = (P, 64, 44)[g]
+            split = (96, 100, 64)[g]
             cast_w1(g, "s", 0, split)
             if split < P:
                 cast_w1(g, "v", split, P, slice(0, 2))
@@ -151,30 +148,44 @@ def tile_picked_sub_mlp_silu_sub_e_kernel(tc, xT, w1, w2, gate, offs, pos1, pos2
                 quant_w1(g, 0, 1)
                 quant_w1(g, 1, 2)
                 quant_w1(g, 2, 4)
+            if g == 0:
+                p_words.append(sb("p_words2", [P, S], U32, tag="w1_grp0"))
+                nc.vector.tensor_copy(p_words[G - 1][:], x_words[G - 1][:].indirect(offs_sb[:]))
             for t in range(4):
-                layer1(acc_a[t][:], t, 0, A, g)
-            for s in range(2):
-                layer1_b(s, 0, g)
-        for s in range(2):
-            for t in range(1, 4):
-                for g in range(G):
-                    layer1_b(s, t, g)
+                layer1(acc_a[t][:], t, 0, A, g, g == 0, g == G - 1)
+            for s in range(slices):
+                for t in (3, 2, 1, 0):
+                    c0 = A + P * s
+                    layer1(acc_h[s][:, t, :], t, c0, c0 + P, g, g == 0 and t == 3, g == G - 1 and t == 0)
 
-        nc.vector.tensor_copy(
-            w2_grp[:].rearrange("p (c i) j -> p c j i", i=4), w2_raw[:].rearrange("p j (c i) -> p c j i", i=4)
-        )
-        nc.vector.quantize_mx(
-            out=w2_words[:].bitcast(FP8X4), scales=w2_bytes[:], in_=w2_grp[:].rearrange("p c j -> p (c j)")
-        )
+        for e in range(2):
+            cols = slice(e * N // 2, (e + 1) * N // 2)
+            nc.vector.tensor_copy(
+                w2_grp[e][:].rearrange("p (c i) j -> p c j i", i=4),
+                w2_raw[:, :, cols].rearrange("p j (c i) -> p c j i", i=4),
+            )
+        for e in range(2):
+            cols = slice(e * N // 2, (e + 1) * N // 2)
+            nc.vector.quantize_mx(
+                out=w2_words[:, cols].bitcast(FP8X4),
+                scales=w2_bytes[:, cols],
+                in_=w2_grp[e][:].rearrange("p c j -> p (c j)"),
+            )
+        h_words = sb("h_words", [P, S], U32, tag="w2_grp1")
+        h_grp_a = sb("h_grp_a", [P, A, 4], BF16, tag="w2_raw")
 
-        for t in range(4):
-            nc.scalar.activation(h_flat[:, t, :], acc_a[t][:], SILU)
-        for s in range(2):
-            nc.scalar.activation(h_grp_b[s][:], acc_b[s][:].rearrange("p t n -> p n t"), SILU)
+        acc_y0 = psum.tile([P, S - 2 * P], F32, name="acc_y0")
 
-        nc.vector.tensor_copy(
-            h_grp_a[:].rearrange("p (c i) t -> p c t i", i=4), h_flat[:].rearrange("p t (c i) -> p c t i", i=4)
-        )
+        def layer2(dst, m, c0, c1):
+            nc.tensor.matmul_mx(
+                out=dst,
+                lhsT=w2_words[:, P * m : P * (m + 1)].bitcast(FP8X4),
+                lhsT_scale=w2_bytes[:, P * m : P * (m + 1)],
+                rhs=h_words[:, c0:c1].bitcast(FP8X4),
+                rhs_scale=h_bytes[:, c0:c1],
+                start=True,
+                stop=True,
+            )
 
         def quant_h(grp, c0, c1):
             nc.vector.quantize_mx(
@@ -183,33 +194,32 @@ def tile_picked_sub_mlp_silu_sub_e_kernel(tc, xT, w1, w2, gate, offs, pos1, pos2
                 in_=grp[:].rearrange("p n t -> p (n t)"),
             )
 
+        for t in range(4):
+            nc.scalar.activation(h_flat[:, t, :], acc_a[t][:], SILU)
+        for s in range(slices):
+            nc.scalar.activation(h_grp[s][:], acc_h[s][:].rearrange("p t n -> p n t"), SILU)
+        nc.vector.tensor_copy(
+            h_grp_a[:].rearrange("p (c i) t -> p c t i", i=4), h_flat[:].rearrange("p t (c i) -> p c t i", i=4)
+        )
         quant_h(h_grp_a, 0, A)
-        for s in range(2):
-            quant_h(h_grp_b[s], A + P * s, A + P * (s + 1))
-
-        tags = ("acc_y0", "acc_y1", "acc_a0", "acc_a1")
-        acc_y = [psum.tile([P, S], F32, name=f"acc_y{m}", tag=tags[m]) for m in range(M_TILES)]
-
-        def layer2(m):
-            for c0, c1 in ((0, A), (A, A + P), (A + P, S)):
-                nc.tensor.matmul_mx(
-                    out=acc_y[m][:, c0:c1],
-                    lhsT=w2_words[:, P * m : P * (m + 1)].bitcast(FP8X4),
-                    lhsT_scale=w2_bytes[:, P * m : P * (m + 1)],
-                    rhs=h_words[:, c0:c1].bitcast(FP8X4),
-                    rhs_scale=h_bytes[:, c0:c1],
-                    start=True,
-                    stop=True,
-                )
-
-        layer2(0)
-        nc.vector.tensor_copy(y_sb[0][:, : A + P], acc_y[0][:, : A + P])
-        nc.scalar.activation(y_sb[0][:, A + P :], acc_y[0][:, A + P :], COPY)
+        layer2(acc_y0[:, 0:A], 0, 0, A)
+        for s in range(slices):
+            c0 = A + P * s
+            quant_h(h_grp[s], c0, c0 + P)
+            if s < slices - 2:
+                layer2(acc_y0[:, c0 : c0 + P], 0, c0, c0 + P)
+        nc.vector.tensor_copy(y_sb[0][:, : S - 2 * P], acc_y0[:])
+        for c0, tag in ((S - 2 * P, "acc_h0"), (S - P, "acc_a0")):
+            acc_late = psum.tile([P, P], F32, name=f"acc_late{c0}", tag=tag)
+            layer2(acc_late[:], 0, c0, c0 + P)
+            nc.scalar.activation(y_sb[0][:, c0 : c0 + P], acc_late[:], COPY)
         for m in range(1, M_TILES):
-            layer2(m)
-            nc.scalar.activation(y_sb[m][:], acc_y[m][:], COPY)
+            acc_y = psum.tile([P, S], F32, name=f"acc_y{m}", tag=f"acc_a{m}")
+            layer2(acc_y[:], m, 0, S)
+            nc.scalar.activation(y_sb[m][:], acc_y[:], COPY)
 
-        sum_tags = ("acc_a2", "acc_a3", "acc_b0", "acc_b1")
+        sum_tags = ("acc_h0", "acc_h1", "acc_h2", "acc_y0")
+        tags = ("acc_a0", "acc_a1", "acc_a2", "acc_a3")
         acc_t = [psum.tile([P, V], F32, name=f"acc_t{m}", tag=sum_tags[m]) for m in range(M_TILES)]
         acc_o = [psum.tile([P, V], F32, name=f"acc_o{m}", tag=tags[m]) for m in range(M_TILES)]
 

@@ -34,9 +34,10 @@ def tile_picked_sub_mlp_silu_sub_e_kernel(tc, xT, w1, w2, gate, offs, pos1, pos2
 
         offs_sb = sb("offs_sb", [P, S // 16], U16)
         pos_sb = [sb(f"pos_sb{d}", [P, V // 16], U16) for d in range(D)]
-        pieces = [(0, 256, "s"), (512, 768, "v"), (256, 512, "s"), (768, 1024, "v")]
-        x_raw = [sb(f"x_raw{g}", [P, 4, T], F32) for g in range(G)]
-        x_grp = [[sb(f"x_grp{g}_{t0}", [P, t1 - t0, 4], BF16) for t0, t1, e in pieces] for g in range(G)]
+        pieces = 4
+        x_raw = [sb(f"x_raw{g}", [P, 4, T], F32) for g in range(G - 1)]
+        x_last = [sb(f"x_last{e}", [P, 4, T // 2], F32) for e in range(2)]
+        x_grp = [[sb(f"x_grp{g}_{i}", [P, 256, 4], BF16) for i in range(pieces)] for g in range(G)]
         x_words = [sb(f"x_words{g}", [P, T], U32) for g in range(G)]
         x_bytes = sb("x_bytes", [P, T], U8)
         p_words = [sb(f"p_words{g}", [P, S], U32) for g in range(G - 1)]
@@ -66,7 +67,9 @@ def tile_picked_sub_mlp_silu_sub_e_kernel(tc, xT, w1, w2, gate, offs, pos1, pos2
         load_x(0)
         nc.sync.dma_start(offs_sb[:], offs)
         load_x(1)
-        load_x(2)
+        for e in range(2):
+            rows = xT[512 * (G - 1) :, e * T // 2 : (e + 1) * T // 2].rearrange("(p j) t -> p j t", j=4)
+            nc.sync.dma_start(out=x_last[e][:], in_=rows)
         for g in range(G):
             nc.sync.dma_start(out=w1_raw[g][:], in_=w1[512 * g : 512 * (g + 1), :].rearrange("(p j) c -> p j c", j=4))
         nc.sync.dma_start(out=w2_raw[:], in_=w2.rearrange("(p j) c -> p j c", j=4))
@@ -79,20 +82,22 @@ def tile_picked_sub_mlp_silu_sub_e_kernel(tc, xT, w1, w2, gate, offs, pos1, pos2
         nc.vector.memset(warm[:], 0.0)
         nc.scalar.activation(warm[:], warm[:], SILU)
 
-        def cast_x(g, i):
-            t0, t1, engine = pieces[i]
-            src = x_raw[g][:, :, t0:t1].rearrange("p j (c i) -> p c j i", i=4)
-            dst = x_grp[g][i][:].rearrange("p (c i) j -> p c j i", i=4)
+        def cast_x(g, i, c0, c1, engine):
+            if g < G - 1:
+                src = x_raw[g][:, :, 256 * i + c0 : 256 * i + c1]
+            else:
+                src = x_last[i // 2][:, :, 256 * (i % 2) + c0 : 256 * (i % 2) + c1]
+            src = src.rearrange("p j (c i) -> p c j i", i=4)
+            dst = x_grp[g][i][:, c0:c1, :].rearrange("p (c i) j -> p c j i", i=4)
             if engine == "v":
                 nc.vector.tensor_copy(dst, src)
             else:
                 nc.scalar.activation(dst, src, COPY)
 
         def quant_x(g, i):
-            t0, t1, engine = pieces[i]
             nc.vector.quantize_mx(
-                out=x_words[g][:, t0:t1].bitcast(FP8X4),
-                scales=x_bytes[4 * g : P, t0:t1],
+                out=x_words[g][:, 256 * i : 256 * (i + 1)].bitcast(FP8X4),
+                scales=x_bytes[4 * g : P, 256 * i : 256 * (i + 1)],
                 in_=x_grp[g][i][:].rearrange("p c j -> p (c j)"),
             )
 
@@ -112,11 +117,15 @@ def tile_picked_sub_mlp_silu_sub_e_kernel(tc, xT, w1, w2, gate, offs, pos1, pos2
             )
 
         for g in range(G):
-            for half in ((0, 1), (2, 3)):
-                for i in half:
-                    cast_x(g, i)
-                for i in half:
-                    quant_x(g, i)
+            extra = (0, 128, 64)[g]
+            cast_x(g, 0, 0, 256, "s")
+            if extra:
+                cast_x(g, 1, 0, extra, "s")
+            cast_x(g, 1, extra, 256, "v")
+            cast_x(g, 2, 0, 256, "s")
+            cast_x(g, 3, 0, 256, "v")
+            for i in range(pieces):
+                quant_x(g, i)
             if g < G - 1:
                 nc.vector.tensor_copy(p_words[g][:], x_words[g][:].indirect(offs_sb[:]))
         nc.vector.tensor_copy(p_bytes[:], x_bytes[:].indirect(offs_sb[:]))
@@ -137,13 +146,14 @@ def tile_picked_sub_mlp_silu_sub_e_kernel(tc, xT, w1, w2, gate, offs, pos1, pos2
             )
 
         for g in range(G):
-            split = (96, 100, 64)[g]
+            split = (78, 100, 56)[g]
             cast_w1(g, "s", 0, split)
             if split < P:
                 cast_w1(g, "v", split, P, slice(0, 2))
                 cast_w1(g, "v", split, P, slice(2, 4))
             if g < 2:
-                quant_w1(g, 0, 4)
+                quant_w1(g, 0, 2)
+                quant_w1(g, 2, 4)
             else:
                 quant_w1(g, 0, 1)
                 quant_w1(g, 1, 2)

@@ -255,17 +255,21 @@ def tile_picked_sub_mlp_silu_sub_e_kernel(tc, xT, w1, w2, gate, offs, pos1, pos2
         def store(m):
             nc.sync.dma_start(out=out[P * m : P * (m + 1), :], in_=sums[m][:])
 
+        def finish(m):
+            nc.vector.tensor_tensor(sums[m][:], acc_o[m][:], terms[m][:, D - 1, :], ADD)
+            store(m)
+
         for m in range(M_TILES):
-            last = D - 1 if m < 2 else D - 2
+            last = D - 1 if m == 0 else D - 2
             for d in range(last + 1):
                 fetch(m, d)
                 turn_and_add(m, d, last)
             turn_back(m)
-            if m < 2:
+            if m == 0:
                 nc.scalar.activation(sums[m][:], acc_o[m][:], COPY)
                 store(m)
-        for m in (2, 3):
+        fetch(1, D - 1)
+        for m in range(2, M_TILES):
             fetch(m, D - 1)
-        for m in (2, 3):
-            nc.vector.tensor_tensor(sums[m][:], acc_o[m][:], terms[m][:, D - 1, :], ADD)
-            store(m)
+            finish(m - 1)
+        finish(M_TILES - 1)

@@ -40,7 +40,7 @@ def tile_picked_sub_mlp_silu_sub_e_kernel(tc, xT, w1, w2, gate, offs, pos1, pos2
         x_grp = [[sb(f"x_grp{g}_{i}", [P, 256, 4], BF16) for i in range(pieces)] for g in range(G)]
         x_words = [sb(f"x_words{g}", [P, T], U32) for g in range(G)]
         x_bytes = sb("x_bytes", [P, T], U8)
-        p_words = [sb(f"p_words{g}", [P, S], U32) for g in range(G - 1)]
+        p_words = [sb(f"p_words{g}", [P, S], U32) for g in range(G)]
         p_bytes = sb("p_bytes", [P, S], U8)
         w1_raw = [sb(f"w1_raw{g}", [P, 4, H], F32) for g in range(G)]
         w1_grp = [sb(f"w1_grp{g}", [P, 4 * H], BF16) for g in range(G)]
@@ -129,6 +129,7 @@ def tile_picked_sub_mlp_silu_sub_e_kernel(tc, xT, w1, w2, gate, offs, pos1, pos2
             if g < G - 1:
                 nc.vector.tensor_copy(p_words[g][:], x_words[g][:].indirect(offs_sb[:]))
         nc.vector.tensor_copy(p_bytes[:], x_bytes[:].indirect(offs_sb[:]))
+        nc.vector.tensor_copy(p_words[G - 1][:], x_words[G - 1][:].indirect(offs_sb[:]))
 
         slices = (S - A) // P
         acc_a = [psum.tile([P, A], F32, name=f"acc_a{t}") for t in range(4)]
@@ -146,7 +147,7 @@ def tile_picked_sub_mlp_silu_sub_e_kernel(tc, xT, w1, w2, gate, offs, pos1, pos2
             )
 
         for g in range(G):
-            split = (78, 100, 56)[g]
+            split = (128, 72, 44)[g]
             cast_w1(g, "s", 0, split)
             if split < P:
                 cast_w1(g, "v", split, P, slice(0, 2))
@@ -157,16 +158,17 @@ def tile_picked_sub_mlp_silu_sub_e_kernel(tc, xT, w1, w2, gate, offs, pos1, pos2
             else:
                 quant_w1(g, 0, 1)
                 quant_w1(g, 1, 2)
-                quant_w1(g, 2, 4)
-            if g == 0:
-                p_words.append(sb("p_words2", [P, S], U32, tag="w1_grp0"))
-                nc.vector.tensor_copy(p_words[G - 1][:], x_words[G - 1][:].indirect(offs_sb[:]))
+                quant_w1(g, 2, 3)
+                quant_w1(g, 3, 4)
             for t in range(4):
                 layer1(acc_a[t][:], t, 0, A, g, g == 0, g == G - 1)
-            for s in range(slices):
+            for s in range(slices if g == 0 else 1):
+                for t in range(4):
+                    layer1(acc_h[s][:, t, :], t, A + P * s, A + P * (s + 1), g, g == 0 and t == 0, g == G - 1 and t == 3)
+        for s in range(1, slices):
+            for g in (2, 1):
                 for t in (3, 2, 1, 0):
-                    c0 = A + P * s
-                    layer1(acc_h[s][:, t, :], t, c0, c0 + P, g, g == 0 and t == 3, g == G - 1 and t == 0)
+                    layer1(acc_h[s][:, t, :], t, A + P * s, A + P * (s + 1), g, False, g == 1 and t == 0)
 
         for e in range(2):
             cols = slice(e * N // 2, (e + 1) * N // 2)

@@ -18,7 +18,6 @@ MULT = mybir.AluOpType.mult
 ADD = mybir.AluOpType.add
 
 P = 128
-A = 128
 G = K // 512
 M_TILES = N // P
 
@@ -50,8 +49,7 @@ def tile_picked_sub_mlp_silu_sub_e_kernel(tc, xT, w1, w2, gate, offs, pos1, pos2
         w2_grp = [sb(f"w2_grp{e}", [P, N // 2, 4], BF16) for e in range(2)]
         w2_words = sb("w2_words", [P, N], U32)
         w2_bytes = sb("w2_bytes", [P, N], U8)
-        h_flat = sb("h_flat", [P, 4, A], BF16)
-        h_grp = [sb(f"h_grp{s}", [P, P, 4], BF16) for s in range((S - A) // P)]
+        h_grp = [sb(f"h_grp{s}", [P, P, 4], BF16) for s in range(S // P)]
         h_bytes = sb("h_bytes", [P, S], U8)
         gates = sb("gates", [P, D, V], F32)
         y_sb = [sb(f"y_sb{m}", [P, S], F32) for m in range(M_TILES)]
@@ -131,8 +129,7 @@ def tile_picked_sub_mlp_silu_sub_e_kernel(tc, xT, w1, w2, gate, offs, pos1, pos2
         nc.vector.tensor_copy(p_bytes[:], x_bytes[:].indirect(offs_sb[:]))
         nc.vector.tensor_copy(p_words[G - 1][:], x_words[G - 1][:].indirect(offs_sb[:]))
 
-        slices = (S - A) // P
-        acc_a = [psum.tile([P, A], F32, name=f"acc_a{t}") for t in range(4)]
+        slices = S // P
         acc_h = [psum.tile([P, 4, P], F32, name=f"acc_h{s}") for s in range(slices)]
 
         def layer1(dst, t, c0, c1, g, start, stop):
@@ -152,23 +149,16 @@ def tile_picked_sub_mlp_silu_sub_e_kernel(tc, xT, w1, w2, gate, offs, pos1, pos2
             if split < P:
                 cast_w1(g, "v", split, P, slice(0, 2))
                 cast_w1(g, "v", split, P, slice(2, 4))
-            if g < 2:
-                quant_w1(g, 0, 2)
-                quant_w1(g, 2, 4)
-            else:
-                quant_w1(g, 0, 1)
-                quant_w1(g, 1, 2)
-                quant_w1(g, 2, 3)
-                quant_w1(g, 3, 4)
-            for t in range(4):
-                layer1(acc_a[t][:], t, 0, A, g, g == 0, g == G - 1)
-            for s in range(slices if g == 0 else 1):
+            quant_w1(g, 0, 2)
+            quant_w1(g, 2, 4)
+            for s in range((slices, 2, 1)[g]):
                 for t in range(4):
-                    layer1(acc_h[s][:, t, :], t, A + P * s, A + P * (s + 1), g, g == 0 and t == 0, g == G - 1 and t == 3)
+                    layer1(acc_h[s][:, t, :], t, P * s, P * (s + 1), g, g == 0 and t == 0, g == G - 1 and t == 3)
         for s in range(1, slices):
-            for g in (2, 1):
+            left = (2,) if s == 1 else (2, 1)
+            for g in left:
                 for t in (3, 2, 1, 0):
-                    layer1(acc_h[s][:, t, :], t, A + P * s, A + P * (s + 1), g, False, g == 1 and t == 0)
+                    layer1(acc_h[s][:, t, :], t, P * s, P * (s + 1), g, False, g == left[-1] and t == 0)
 
         for e in range(2):
             cols = slice(e * N // 2, (e + 1) * N // 2)
@@ -184,7 +174,6 @@ def tile_picked_sub_mlp_silu_sub_e_kernel(tc, xT, w1, w2, gate, offs, pos1, pos2
                 in_=w2_grp[e][:].rearrange("p c j -> p (c j)"),
             )
         h_words = sb("h_words", [P, S], U32, tag="w2_grp1")
-        h_grp_a = sb("h_grp_a", [P, A, 4], BF16, tag="w2_raw")
 
         acc_y0 = psum.tile([P, S - 2 * P], F32, name="acc_y0")
 
@@ -206,32 +195,25 @@ def tile_picked_sub_mlp_silu_sub_e_kernel(tc, xT, w1, w2, gate, offs, pos1, pos2
                 in_=grp[:].rearrange("p n t -> p (n t)"),
             )
 
-        for t in range(4):
-            nc.scalar.activation(h_flat[:, t, :], acc_a[t][:], SILU)
         for s in range(slices):
             nc.scalar.activation(h_grp[s][:], acc_h[s][:].rearrange("p t n -> p n t"), SILU)
-        nc.vector.tensor_copy(
-            h_grp_a[:].rearrange("p (c i) t -> p c t i", i=4), h_flat[:].rearrange("p t (c i) -> p c t i", i=4)
-        )
-        quant_h(h_grp_a, 0, A)
-        layer2(acc_y0[:, 0:A], 0, 0, A)
         for s in range(slices):
-            c0 = A + P * s
+            c0 = P * s
             quant_h(h_grp[s], c0, c0 + P)
             if s < slices - 2:
                 layer2(acc_y0[:, c0 : c0 + P], 0, c0, c0 + P)
         nc.vector.tensor_copy(y_sb[0][:, : S - 2 * P], acc_y0[:])
-        for c0, tag in ((S - 2 * P, "acc_h0"), (S - P, "acc_a0")):
+        for c0, tag in ((S - 2 * P, "acc_h0"), (S - P, "acc_b0")):
             acc_late = psum.tile([P, P], F32, name=f"acc_late{c0}", tag=tag)
             layer2(acc_late[:], 0, c0, c0 + P)
             nc.scalar.activation(y_sb[0][:, c0 : c0 + P], acc_late[:], COPY)
         for m in range(1, M_TILES):
-            acc_y = psum.tile([P, S], F32, name=f"acc_y{m}", tag=f"acc_a{m}")
+            acc_y = psum.tile([P, S], F32, name=f"acc_y{m}", tag=("acc_b1", "acc_b2", "acc_h1")[m - 1])
             layer2(acc_y[:], m, 0, S)
             nc.scalar.activation(y_sb[m][:], acc_y[:], COPY)
 
-        sum_tags = ("acc_h0", "acc_h1", "acc_h2", "acc_y0")
-        tags = ("acc_a0", "acc_a1", "acc_a2", "acc_a3")
+        sum_tags = ("acc_h2", "acc_h3", "acc_y0", "acc_h0")
+        tags = ("acc_b0", "acc_b1", "acc_b2", "acc_h1")
         acc_t = [psum.tile([P, V], F32, name=f"acc_t{m}", tag=sum_tags[m]) for m in range(M_TILES)]
         acc_o = [psum.tile([P, V], F32, name=f"acc_o{m}", tag=tags[m]) for m in range(M_TILES)]
 

@@ -20,6 +20,7 @@ ADD = mybir.AluOpType.add
 P = 128
 G = K // 512
 M_TILES = N // P
+X_SHARE = ((256, 384), (640, 512), (640, 512))
 
 
 def tile_picked_sub_mlp_silu_sub_e_kernel(tc, xT, w1, w2, gate, offs, pos1, pos2, pos3, pos4, out):
@@ -34,8 +35,7 @@ def tile_picked_sub_mlp_silu_sub_e_kernel(tc, xT, w1, w2, gate, offs, pos1, pos2
         offs_sb = sb("offs_sb", [P, S // 16], U16)
         pos_sb = [sb(f"pos_sb{d}", [P, V // 16], U16) for d in range(D)]
         pieces = 4
-        x_raw = [sb(f"x_raw{g}", [P, 4, T], F32) for g in range(G - 1)]
-        x_last = [sb(f"x_last{e}", [P, 4, T // 2], F32) for e in range(2)]
+        x_raw = [[sb(f"x_raw{g}_{e}", [P, 2, T], F32) for e in range(2)] for g in range(G)]
         x_grp = [[sb(f"x_grp{g}_{i}", [P, 256, 4], BF16) for i in range(pieces)] for g in range(G)]
         x_words = [sb(f"x_words{g}", [P, T], U32) for g in range(G)]
         x_bytes = sb("x_bytes", [P, T], U8)
@@ -59,15 +59,12 @@ def tile_picked_sub_mlp_silu_sub_e_kernel(tc, xT, w1, w2, gate, offs, pos1, pos2
         sums = [sb(f"sums{m}", [P, V], F32) for m in range(M_TILES)]
         warm = sb("warm", [P, 1], F32)
 
-        def load_x(g):
-            nc.sync.dma_start(out=x_raw[g][:], in_=xT[512 * g : 512 * (g + 1), :].rearrange("(p j) t -> p j t", j=4))
-
-        load_x(0)
-        nc.sync.dma_start(offs_sb[:], offs)
-        load_x(1)
-        for e in range(2):
-            rows = xT[512 * (G - 1) :, e * T // 2 : (e + 1) * T // 2].rearrange("(p j) t -> p j t", j=4)
-            nc.sync.dma_start(out=x_last[e][:], in_=rows)
+        for g in range(G):
+            rows = xT[512 * g : 512 * (g + 1), :].rearrange("(p j) t -> p j t", j=4)
+            for e in range(2):
+                nc.sync.dma_start(out=x_raw[g][e][:], in_=rows[:, 2 * e : 2 * e + 2, :])
+            if g == 0:
+                nc.sync.dma_start(offs_sb[:], offs)
         for g in range(G):
             nc.sync.dma_start(out=w1_raw[g][:], in_=w1[512 * g : 512 * (g + 1), :].rearrange("(p j) c -> p j c", j=4))
         nc.sync.dma_start(out=w2_raw[:], in_=w2.rearrange("(p j) c -> p j c", j=4))
@@ -80,13 +77,9 @@ def tile_picked_sub_mlp_silu_sub_e_kernel(tc, xT, w1, w2, gate, offs, pos1, pos2
         nc.vector.memset(warm[:], 0.0)
         nc.scalar.activation(warm[:], warm[:], SILU)
 
-        def cast_x(g, i, c0, c1, engine):
-            if g < G - 1:
-                src = x_raw[g][:, :, 256 * i + c0 : 256 * i + c1]
-            else:
-                src = x_last[i // 2][:, :, 256 * (i % 2) + c0 : 256 * (i % 2) + c1]
-            src = src.rearrange("p j (c i) -> p c j i", i=4)
-            dst = x_grp[g][i][:, c0:c1, :].rearrange("p (c i) j -> p c j i", i=4)
+        def cast_x(g, e, i, c0, c1, engine):
+            src = x_raw[g][e][:, :, 256 * i + c0 : 256 * i + c1].rearrange("p j (c i) -> p c j i", i=4)
+            dst = x_grp[g][i][:, c0:c1, 2 * e : 2 * e + 2].rearrange("p (c i) j -> p c j i", i=4)
             if engine == "v":
                 nc.vector.tensor_copy(dst, src)
             else:
@@ -115,13 +108,14 @@ def tile_picked_sub_mlp_silu_sub_e_kernel(tc, xT, w1, w2, gate, offs, pos1, pos2
             )
 
         for g in range(G):
-            extra = (0, 128, 64)[g]
-            cast_x(g, 0, 0, 256, "s")
-            if extra:
-                cast_x(g, 1, 0, extra, "s")
-            cast_x(g, 1, extra, 256, "v")
-            cast_x(g, 2, 0, 256, "s")
-            cast_x(g, 3, 0, 256, "v")
+            for e in range(2):
+                border = T - X_SHARE[g][e]
+                for i in range(pieces):
+                    cut = min(max(border - 256 * i, 0), 256)
+                    if cut > 0:
+                        cast_x(g, e, i, 0, cut, "v")
+                    if cut < 256:
+                        cast_x(g, e, i, cut, 256, "s")
             for i in range(pieces):
                 quant_x(g, i)
             if g < G - 1:

@@ -57,7 +57,6 @@ def tile_picked_sub_mlp_silu_sub_e_kernel(tc, xT, w1, w2, gate, offs, pos1, pos2
         turned = [sb(f"turned{m}", [P, V], F32) for m in range(M_TILES)]
         ident = sb("ident", [P, P], F32)
         sums = [sb(f"sums{m}", [P, V], F32) for m in range(M_TILES)]
-        warm = sb("warm", [P, 1], F32)
 
         for g in range(G):
             rows = xT[512 * g : 512 * (g + 1), :].rearrange("(p j) t -> p j t", j=4)
@@ -74,8 +73,6 @@ def tile_picked_sub_mlp_silu_sub_e_kernel(tc, xT, w1, w2, gate, offs, pos1, pos2
 
         nc.gpsimd.memset(x_bytes[:], 0)
         make_identity(nc, ident[:])
-        nc.vector.memset(warm[:], 0.0)
-        nc.scalar.activation(warm[:], warm[:], SILU)
 
         def cast_x(g, e, i, c0, c1, engine):
             src = x_raw[g][e][:, :, 256 * i + c0 : 256 * i + c1].rearrange("p j (c i) -> p c j i", i=4)
@@ -138,7 +135,7 @@ def tile_picked_sub_mlp_silu_sub_e_kernel(tc, xT, w1, w2, gate, offs, pos1, pos2
             )
 
         for g in range(G):
-            split = (128, 72, 44)[g]
+            split = (128, 84, 48)[g]
             cast_w1(g, "s", 0, split)
             if split < P:
                 cast_w1(g, "v", split, P, slice(0, 2))

@@ -203,48 +203,63 @@ def tile_picked_sub_mlp_silu_sub_e_kernel(tc, xT, w1, w2, gate, offs, pos1, pos2
             layer2(acc_y[:], m, 0, S)
             nc.scalar.activation(y_sb[m][:], acc_y[:], COPY)
 
-        sum_tags = ("acc_h2", "acc_h3", "acc_y0", "acc_h0")
-        tags = ("acc_b0", "acc_b1", "acc_b2", "acc_h1")
-        acc_t = [psum.tile([P, V], F32, name=f"acc_t{m}", tag=sum_tags[m]) for m in range(M_TILES)]
-        acc_o = [psum.tile([P, V], F32, name=f"acc_o{m}", tag=tags[m]) for m in range(M_TILES)]
+        last_tile = M_TILES - 1
+        sum_tags = ("acc_h2", "acc_h3", "acc_y0")
+        back_tags = ("acc_b0", "acc_b1", "acc_b2")
+        acc_t = [psum.tile([P, V], F32, name=f"acc_t{m}", tag=sum_tags[m]) for m in range(last_tile)]
+        acc_o = [psum.tile([P, V], F32, name=f"acc_o{m}", tag=back_tags[m]) for m in range(last_tile)]
 
-        def fetch(m, d):
-            nc.vector.tensor_tensor(terms[m][:, d, :], y_sb[m][:].indirect(pos_sb[d][:]), gates[:, d, :], MULT)
+        def fetch(m, d, u0=0, u1=V // P):
+            nc.vector.tensor_tensor(
+                terms[m][:, d, P * u0 : P * u1],
+                y_sb[m][:].indirect(pos_sb[d][:, 8 * u0 : 8 * u1]),
+                gates[:, d, P * u0 : P * u1],
+                MULT,
+            )
 
-        def turn_and_add(m, d, last):
-            for u in range(V // P):
-                nc.tensor.matmul(
-                    acc_t[m][:, P * u : P * (u + 1)],
-                    lhsT=terms[m][:, d, P * u : P * (u + 1)],
-                    rhs=ident[:],
-                    start=(d == 0 and u == 0),
-                    stop=(d == last and u == V // P - 1),
-                    is_transpose=True,
-                )
+        def turn_and_add(dst, m, d, u, start, stop):
+            nc.tensor.matmul(
+                dst,
+                lhsT=terms[m][:, d, P * u : P * (u + 1)],
+                rhs=ident[:],
+                start=start,
+                stop=stop,
+                is_transpose=True,
+            )
 
-        def turn_back(m):
+        def store(m, c0, c1):
+            nc.sync.dma_start(out=out[P * m : P * (m + 1), c0:c1], in_=sums[m][:, c0:c1])
+
+        for m in range(last_tile):
+            last = D - 1 if m < last_tile - 1 else D - 2
+            for d in range(last + 1):
+                fetch(m, d)
+                for u in range(V // P):
+                    turn_and_add(acc_t[m][:, P * u : P * (u + 1)], m, d, u, d == 0 and u == 0, d == last and u == V // P - 1)
             nc.scalar.activation(turned[m][:], acc_t[m][:], COPY)
             for u in range(V // P):
                 nc.tensor.transpose(acc_o[m][:, P * u : P * (u + 1)], turned[m][:, P * u : P * (u + 1)], ident[:])
-
-        def store(m):
-            nc.sync.dma_start(out=out[P * m : P * (m + 1), :], in_=sums[m][:])
-
-        def finish(m):
-            nc.vector.tensor_tensor(sums[m][:], acc_o[m][:], terms[m][:, D - 1, :], ADD)
-            store(m)
-
-        for m in range(M_TILES):
-            last = D - 1 if m == 0 else D - 2
-            for d in range(last + 1):
-                fetch(m, d)
-                turn_and_add(m, d, last)
-            turn_back(m)
-            if m == 0:
+            if last == D - 1:
                 nc.scalar.activation(sums[m][:], acc_o[m][:], COPY)
-                store(m)
-        fetch(1, D - 1)
-        for m in range(2, M_TILES):
-            fetch(m, D - 1)
-            finish(m - 1)
-        finish(M_TILES - 1)
+                store(m, 0, V)
+
+        m = last_tile
+        half_t = [psum.tile([P, P], F32, name=f"half_t{u}", tag=("acc_h0", "acc_h2")[u]) for u in range(V // P)]
+        half_o = [psum.tile([P, P], F32, name=f"half_o{u}", tag=("acc_h1", "acc_b0")[u]) for u in range(V // P)]
+        for d in range(D - 2):
+            fetch(m, d)
+            for u in range(V // P):
+                turn_and_add(half_t[u][:], m, d, u, d == 0, False)
+        for u in range(V // P):
+            fetch(m, D - 2, u, u + 1)
+            turn_and_add(half_t[u][:], m, D - 2, u, False, True)
+            nc.scalar.activation(turned[m][:, P * u : P * (u + 1)], half_t[u][:], COPY)
+            nc.tensor.transpose(half_o[u][:], turned[m][:, P * u : P * (u + 1)], ident[:])
+        fetch(m - 1, D - 1)
+        fetch(m, D - 1)
+        nc.vector.tensor_tensor(sums[m - 1][:], acc_o[m - 1][:], terms[m - 1][:, D - 1, :], ADD)
+        store(m - 1, 0, V)
+        for u in range(V // P):
+            cols = slice(P * u, P * (u + 1))
+            nc.vector.tensor_tensor(sums[m][:, cols], half_o[u][:], terms[m][:, D - 1, cols], ADD)
+            store(m, P * u, P * (u + 1))

@@ -21,6 +21,7 @@ P = 128
 G = K // 512
 M_TILES = N // P
 X_SHARE = ((256, 384), (640, 512), (640, 512))
+W1_SHARE = ((64, 64), (42, 42), (0, 48))
 
 
 def tile_picked_sub_mlp_silu_sub_e_kernel(tc, xT, w1, w2, gate, offs, pos1, pos2, pos3, pos4, out):
@@ -66,7 +67,9 @@ def tile_picked_sub_mlp_silu_sub_e_kernel(tc, xT, w1, w2, gate, offs, pos1, pos2
                 nc.sync.dma_start(offs_sb[:], offs)
         for g in range(G):
             nc.sync.dma_start(out=w1_raw[g][:], in_=w1[512 * g : 512 * (g + 1), :].rearrange("(p j) c -> p j c", j=4))
-        nc.sync.dma_start(out=w2_raw[:], in_=w2.rearrange("(p j) c -> p j c", j=4))
+        w2_rows = w2.rearrange("(a u i e) c -> i a u (e c)", u=2, i=2, e=2)
+        for i in range(2):
+            nc.sync.dma_start(out=w2_raw[i:P:2, :, :].rearrange("p (u e) c -> p u (e c)", u=2), in_=w2_rows[i])
         for d, pos in enumerate((pos1, pos2, pos3, pos4)):
             nc.sync.dma_start(pos_sb[d][:], pos)
         nc.sync.dma_start(out=gates[:], in_=gate[:, 0:P, :].rearrange("d p v -> p d v"))
@@ -89,13 +92,13 @@ def tile_picked_sub_mlp_silu_sub_e_kernel(tc, xT, w1, w2, gate, offs, pos1, pos2
                 in_=x_grp[g][i][:].rearrange("p c j -> p (c j)"),
             )
 
-        def cast_w1(g, engine, m0, m1, ts=slice(0, 4)):
-            src = w1_raw[g][:].rearrange("p j (m t) -> p m j t", t=4)[:, m0:m1, :, ts]
-            dst = w1_grp[g][:].rearrange("p (t m j) -> p m j t", t=4, j=4)[:, m0:m1, :, ts]
+        def cast_w1(g, engine, u, a0, a1):
+            src = w1_raw[g][:].rearrange("p j (a u i e) -> p u a j i e", u=2, i=2, e=2)[:, u, a0:a1]
+            dst = w1_grp[g][:].rearrange("p (u e a i j) -> p u a j i e", u=2, e=2, i=2, j=4)[:, u, a0:a1]
             if engine == "v":
                 nc.vector.tensor_copy(dst, src)
             else:
-                nc.scalar.activation(dst, src, COPY)
+                nc.scalar.copy(dst, src)
 
         def quant_w1(g, t0, t1):
             nc.vector.quantize_mx(
@@ -135,11 +138,12 @@ def tile_picked_sub_mlp_silu_sub_e_kernel(tc, xT, w1, w2, gate, offs, pos1, pos2
             )
 
         for g in range(G):
-            split = (128, 84, 48)[g]
-            cast_w1(g, "s", 0, split)
-            if split < P:
-                cast_w1(g, "v", split, P, slice(0, 2))
-                cast_w1(g, "v", split, P, slice(2, 4))
+            for u in range(2):
+                split = W1_SHARE[g][u]
+                if split > 0:
+                    cast_w1(g, "s", u, 0, split)
+                if split < P // 2:
+                    cast_w1(g, "v", u, split, P // 2)
             quant_w1(g, 0, 2)
             quant_w1(g, 2, 4)
             for s in range((slices, 2, 1)[g]):

@@ -43,11 +43,11 @@ def tile_picked_sub_mlp_silu_sub_e_kernel(tc, xT, w1, w2, gate, offs, pos1, pos2
         p_words = [sb(f"p_words{g}", [P, S], U32) for g in range(G)]
         p_bytes = sb("p_bytes", [P, S], U8)
         w1_raw = [sb(f"w1_raw{g}", [P, 4, H], F32) for g in range(G)]
-        w1_grp = [sb(f"w1_grp{g}", [P, 4 * H], BF16) for g in range(G)]
+        w1_grp = [[sb(f"w1_grp{g}_{u}", [P, 2 * H], BF16) for u in range(2)] for g in range(G)]
         w1_words = [sb(f"w1_words{g}", [P, H], U32) for g in range(G)]
         w1_bytes = [sb(f"w1_bytes{g}", [P, H], U8) for g in range(G)]
         w2_raw = sb("w2_raw", [P, 4, N], F32)
-        w2_grp = [sb(f"w2_grp{e}", [P, N // 2, 4], BF16) for e in range(2)]
+        w2_grp = [sb(f"w2_grp{e}", [P, P, 4], BF16) for e in range(M_TILES - 1)]
         w2_words = sb("w2_words", [P, N], U32)
         w2_bytes = sb("w2_bytes", [P, N], U8)
         h_grp = [sb(f"h_grp{s}", [P, P, 4], BF16) for s in range(S // P)]
@@ -94,7 +94,7 @@ def tile_picked_sub_mlp_silu_sub_e_kernel(tc, xT, w1, w2, gate, offs, pos1, pos2
 
         def cast_w1(g, engine, u, a0, a1):
             src = w1_raw[g][:].rearrange("p j (a u i e) -> p u a j i e", u=2, i=2, e=2)[:, u, a0:a1]
-            dst = w1_grp[g][:].rearrange("p (u e a i j) -> p u a j i e", u=2, e=2, i=2, j=4)[:, u, a0:a1]
+            dst = w1_grp[g][u][:].rearrange("p (e a i j) -> p a j i e", e=2, i=2, j=4)[:, a0:a1]
             if engine == "v":
                 nc.vector.tensor_copy(dst, src)
             else:
@@ -104,7 +104,7 @@ def tile_picked_sub_mlp_silu_sub_e_kernel(tc, xT, w1, w2, gate, offs, pos1, pos2
             nc.vector.quantize_mx(
                 out=w1_words[g][:, P * t0 : P * t1].bitcast(FP8X4),
                 scales=w1_bytes[g][:, P * t0 : P * t1],
-                in_=w1_grp[g][:, 512 * t0 : 512 * t1],
+                in_=w1_grp[g][t0 // 2][:],
             )
 
         for g in range(G):
@@ -146,31 +146,35 @@ def tile_picked_sub_mlp_silu_sub_e_kernel(tc, xT, w1, w2, gate, offs, pos1, pos2
                     cast_w1(g, "v", u, split, P // 2)
             quant_w1(g, 0, 2)
             quant_w1(g, 2, 4)
-            for s in range((slices, 2, 1)[g]):
+            for s in range((slices, 1, 1)[g]):
                 for t in range(4):
                     layer1(acc_h[s][:, t, :], t, P * s, P * (s + 1), g, g == 0 and t == 0, g == G - 1 and t == 3)
         for s in range(1, slices):
-            left = (2,) if s == 1 else (2, 1)
+            left = (2, 1)
             for g in left:
                 for t in (3, 2, 1, 0):
                     layer1(acc_h[s][:, t, :], t, P * s, P * (s + 1), g, False, g == left[-1] and t == 0)
 
-        for e in range(2):
-            cols = slice(e * N // 2, (e + 1) * N // 2)
+        def cast_w2(grp, m):
             nc.vector.tensor_copy(
-                w2_grp[e][:].rearrange("p (c i) j -> p c j i", i=4),
-                w2_raw[:, :, cols].rearrange("p j (c i) -> p c j i", i=4),
+                grp[:].rearrange("p (c i) j -> p c j i", i=4),
+                w2_raw[:, :, P * m : P * (m + 1)].rearrange("p j (c i) -> p c j i", i=4),
             )
-        for e in range(2):
-            cols = slice(e * N // 2, (e + 1) * N // 2)
-            nc.vector.quantize_mx(
-                out=w2_words[:, cols].bitcast(FP8X4),
-                scales=w2_bytes[:, cols],
-                in_=w2_grp[e][:].rearrange("p c j -> p (c j)"),
-            )
-        h_words = sb("h_words", [P, S], U32, tag="w2_grp1")
 
-        acc_y0 = psum.tile([P, S - 2 * P], F32, name="acc_y0")
+        def quant_w2(grp, m):
+            nc.vector.quantize_mx(
+                out=w2_words[:, P * m : P * (m + 1)].bitcast(FP8X4),
+                scales=w2_bytes[:, P * m : P * (m + 1)],
+                in_=grp[:].rearrange("p c j -> p (c j)"),
+            )
+
+        for m in range(M_TILES - 1):
+            cast_w2(w2_grp[m], m)
+        for m in range(M_TILES - 1):
+            quant_w2(w2_grp[m], m)
+        h_words = sb("h_words", [P, S], U32, tag="w2_grp2")
+
+        acc_y0 = psum.tile([P, S - P], F32, name="acc_y0")
 
         def layer2(dst, m, c0, c1):
             nc.tensor.matmul_mx(
@@ -195,10 +199,13 @@ def tile_picked_sub_mlp_silu_sub_e_kernel(tc, xT, w1, w2, gate, offs, pos1, pos2
         for s in range(slices):
             c0 = P * s
             quant_h(h_grp[s], c0, c0 + P)
-            if s < slices - 2:
+            if s < slices - 1:
                 layer2(acc_y0[:, c0 : c0 + P], 0, c0, c0 + P)
-        nc.vector.tensor_copy(y_sb[0][:, : S - 2 * P], acc_y0[:])
-        for c0, tag in ((S - 2 * P, "acc_h0"), (S - P, "acc_b0")):
+        w2_late = sb("w2_late", [P, P, 4], BF16, tag="h_grp3")
+        cast_w2(w2_late, M_TILES - 1)
+        nc.scalar.activation(y_sb[0][:, : S - P], acc_y0[:], COPY)
+        quant_w2(w2_late, M_TILES - 1)
+        for c0, tag in ((S - P, "acc_b0"),):
             acc_late = psum.tile([P, P], F32, name=f"acc_late{c0}", tag=tag)
             layer2(acc_late[:], 0, c0, c0 + P)
             nc.scalar.activation(y_sb[0][:, c0 : c0 + P], acc_late[:], COPY)

@@ -40,7 +40,7 @@ def tile_picked_sub_mlp_silu_sub_e_kernel(tc, xT, w1, w2, gate, offs, pos1, pos2
         x_grp = [[sb(f"x_grp{g}_{i}", [P, 256, 4], BF16) for i in range(pieces)] for g in range(G)]
         x_words = [sb(f"x_words{g}", [P, T], U32) for g in range(G)]
         x_bytes = sb("x_bytes", [P, T], U8)
-        p_words = [sb(f"p_words{g}", [P, S], U32) for g in range(G)]
+        p_words = [sb(f"p_words{g}", [P, S if g < G - 1 else S // 2], U32) for g in range(G)]
         p_bytes = sb("p_bytes", [P, S], U8)
         w1_raw = [sb(f"w1_raw{g}", [P, 4, H], F32) for g in range(G)]
         w1_grp = [[sb(f"w1_grp{g}_{u}", [P, 2 * H], BF16) for u in range(2)] for g in range(G)]
@@ -76,6 +76,9 @@ def tile_picked_sub_mlp_silu_sub_e_kernel(tc, xT, w1, w2, gate, offs, pos1, pos2
 
         nc.gpsimd.memset(x_bytes[:], 0)
         make_identity(nc, ident[:])
+        warm = sb("warm", [P, 2], F32)
+        nc.vector.memset(warm[:, 0:1], 0.0)
+        nc.scalar.activation(warm[:, 1:2], warm[:, 0:1], SILU)
 
         def cast_x(g, e, i, c0, c1, engine):
             src = x_raw[g][e][:, :, 256 * i + c0 : 256 * i + c1].rearrange("p j (c i) -> p c j i", i=4)
@@ -121,17 +124,22 @@ def tile_picked_sub_mlp_silu_sub_e_kernel(tc, xT, w1, w2, gate, offs, pos1, pos2
             if g < G - 1:
                 nc.vector.tensor_copy(p_words[g][:], x_words[g][:].indirect(offs_sb[:]))
         nc.vector.tensor_copy(p_bytes[:], x_bytes[:].indirect(offs_sb[:]))
-        nc.vector.tensor_copy(p_words[G - 1][:], x_words[G - 1][:].indirect(offs_sb[:]))
+        nc.vector.tensor_copy(p_words[G - 1][:], x_words[G - 1][:].indirect(offs_sb[:, : S // 32]))
 
         slices = S // P
+        late_words = []
         acc_h = [psum.tile([P, 4, P], F32, name=f"acc_h{s}") for s in range(slices)]
 
         def layer1(dst, t, c0, c1, g, start, stop):
+            if g == G - 1 and c0 >= S // 2:
+                words = late_words[0][:, c0 - S // 2 : c1 - S // 2]
+            else:
+                words = p_words[g][:, c0:c1]
             nc.tensor.matmul_mx(
                 out=dst,
                 lhsT=w1_words[g][:, P * t : P * (t + 1)].bitcast(FP8X4),
                 lhsT_scale=w1_bytes[g][:, P * t : P * (t + 1)],
-                rhs=p_words[g][:, c0:c1].bitcast(FP8X4),
+                rhs=words.bitcast(FP8X4),
                 rhs_scale=p_bytes[4 * g : P, c0:c1],
                 start=start,
                 stop=stop,
@@ -146,11 +154,13 @@ def tile_picked_sub_mlp_silu_sub_e_kernel(tc, xT, w1, w2, gate, offs, pos1, pos2
                     cast_w1(g, "v", u, split, P // 2)
             quant_w1(g, 0, 2)
             quant_w1(g, 2, 4)
-            for s in range((slices, 1, 1)[g]):
+            for s in range((slices, slices - 1, 1)[g]):
                 for t in range(4):
                     layer1(acc_h[s][:, t, :], t, P * s, P * (s + 1), g, g == 0 and t == 0, g == G - 1 and t == 3)
+        late_words.append(sb("late_words", [P, S // 2], U32, tag=f"w1_grp{G - 1}_1"))
+        nc.vector.tensor_copy(late_words[0][:], x_words[G - 1][:].indirect(offs_sb[:, S // 32 :]))
         for s in range(1, slices):
-            left = (2, 1)
+            left = (2,) if s < slices - 1 else (2, 1)
             for g in left:
                 for t in (3, 2, 1, 0):
                     layer1(acc_h[s][:, t, :], t, P * s, P * (s + 1), g, False, g == left[-1] and t == 0)

@@ -47,10 +47,12 @@ def tile_picked_sub_mlp_silu_sub_e_kernel(tc, xT, w1, w2, gate, offs, pos1, pos2
         w1_words = [sb(f"w1_words{g}", [P, H], U32) for g in range(G)]
         w1_bytes = [sb(f"w1_bytes{g}", [P, H], U8) for g in range(G)]
         w2_raw = sb("w2_raw", [P, 4, N], F32)
-        w2_grp = [sb(f"w2_grp{e}", [P, P, 4], BF16) for e in range(M_TILES - 1)]
-        w2_words = sb("w2_words", [P, N], U32)
+        w2_cuts = ((0, 128), (128, 256), (256, 512))
+        w2_grp = [sb(f"w2_grp{e}", [P, c1 - c0, 4], BF16) for e, (c0, c1) in enumerate(w2_cuts)]
+        w2_words = [sb("w2_words", [P, P], U32)[:]]
         w2_bytes = sb("w2_bytes", [P, N], U8)
-        h_grp = [sb(f"h_grp{s}", [P, P, 4], BF16) for s in range(S // P)]
+        h_cuts = ((0, 256), (256, 384), (384, 448), (448, 512))
+        h_grp = [sb(f"h_grp{s}", [P, c1 - c0, 4], BF16) for s, (c0, c1) in enumerate(h_cuts)]
         h_bytes = sb("h_bytes", [P, S], U8)
         gates = sb("gates", [P, D, V], F32)
         y_sb = [sb(f"y_sb{m}", [P, S], F32) for m in range(M_TILES)]
@@ -165,31 +167,33 @@ def tile_picked_sub_mlp_silu_sub_e_kernel(tc, xT, w1, w2, gate, offs, pos1, pos2
                 for t in (3, 2, 1, 0):
                     layer1(acc_h[s][:, t, :], t, P * s, P * (s + 1), g, False, g == left[-1] and t == 0)
 
-        def cast_w2(grp, m):
+        def cast_w2(part):
+            c0, c1 = w2_cuts[part]
             nc.vector.tensor_copy(
-                grp[:].rearrange("p (c i) j -> p c j i", i=4),
-                w2_raw[:, :, P * m : P * (m + 1)].rearrange("p j (c i) -> p c j i", i=4),
+                w2_grp[part][:].rearrange("p (c i) j -> p c j i", i=4),
+                w2_raw[:, :, c0:c1].rearrange("p j (c i) -> p c j i", i=4),
             )
 
-        def quant_w2(grp, m):
+        def quant_w2(part, words):
+            c0, c1 = w2_cuts[part]
             nc.vector.quantize_mx(
-                out=w2_words[:, P * m : P * (m + 1)].bitcast(FP8X4),
-                scales=w2_bytes[:, P * m : P * (m + 1)],
-                in_=grp[:].rearrange("p c j -> p (c j)"),
+                out=words.bitcast(FP8X4),
+                scales=w2_bytes[:, c0:c1],
+                in_=w2_grp[part][:].rearrange("p c j -> p (c j)"),
             )
 
-        for m in range(M_TILES - 1):
-            cast_w2(w2_grp[m], m)
-        for m in range(M_TILES - 1):
-            quant_w2(w2_grp[m], m)
-        h_words = sb("h_words", [P, S], U32, tag="w2_grp2")
+        cast_w2(0)
+        cast_w2(1)
+        quant_w2(0, w2_words[0])
+        cast_w2(2)
+        h_words = sb("h_words", [P, S], U32, tag="w2_grp0")
 
-        acc_y0 = psum.tile([P, S - P], F32, name="acc_y0")
+        acc_y0 = psum.tile([P, 2 * P], F32, name="acc_y0")
 
         def layer2(dst, m, c0, c1):
             nc.tensor.matmul_mx(
                 out=dst,
-                lhsT=w2_words[:, P * m : P * (m + 1)].bitcast(FP8X4),
+                lhsT=w2_words[m].bitcast(FP8X4),
                 lhsT_scale=w2_bytes[:, P * m : P * (m + 1)],
                 rhs=h_words[:, c0:c1].bitcast(FP8X4),
                 rhs_scale=h_bytes[:, c0:c1],
@@ -204,21 +208,24 @@ def tile_picked_sub_mlp_silu_sub_e_kernel(tc, xT, w1, w2, gate, offs, pos1, pos2
                 in_=grp[:].rearrange("p n t -> p (n t)"),
             )
 
-        for s in range(slices):
-            nc.scalar.activation(h_grp[s][:], acc_h[s][:].rearrange("p t n -> p n t"), SILU)
-        for s in range(slices):
-            c0 = P * s
-            quant_h(h_grp[s], c0, c0 + P)
-            if s < slices - 1:
-                layer2(acc_y0[:, c0 : c0 + P], 0, c0, c0 + P)
-        w2_late = sb("w2_late", [P, P, 4], BF16, tag="h_grp3")
-        cast_w2(w2_late, M_TILES - 1)
-        nc.scalar.activation(y_sb[0][:, : S - P], acc_y0[:], COPY)
-        quant_w2(w2_late, M_TILES - 1)
-        for c0, tag in ((S - P, "acc_b0"),):
-            acc_late = psum.tile([P, P], F32, name=f"acc_late{c0}", tag=tag)
-            layer2(acc_late[:], 0, c0, c0 + P)
-            nc.scalar.activation(y_sb[0][:, c0 : c0 + P], acc_late[:], COPY)
+        for s, (c0, c1) in enumerate(h_cuts):
+            for b0 in range(c0, c1, P):
+                b1 = min(b0 + P, c1)
+                src = acc_h[b0 // P][:, :, b0 % P : b0 % P + b1 - b0]
+                nc.scalar.activation(h_grp[s][:, b0 - c0 : b1 - c0, :], src.rearrange("p t n -> p n t"), SILU)
+        for s, (c0, c1) in enumerate(h_cuts):
+            quant_h(h_grp[s], c0, c1)
+            if s == 0:
+                layer2(acc_y0[:], 0, c0, c1)
+        w2_late = sb("w2_late", [P, N - P], U32, tag=f"h_grp{len(h_cuts) - 1}")
+        w2_words.extend(w2_late[:, P * m : P * (m + 1)] for m in range(M_TILES - 1))
+        quant_w2(1, w2_late[:, :P])
+        quant_w2(2, w2_late[:, P:])
+        nc.scalar.activation(y_sb[0][:, : 2 * P], acc_y0[:], COPY)
+        for (c0, c1), tag in zip(h_cuts[1:], ("acc_h0", "acc_b0", "acc_h1")):
+            acc_late = psum.tile([P, c1 - c0], F32, name=f"acc_late{c0}", tag=tag)
+            layer2(acc_late[:], 0, c0, c1)
+            nc.scalar.activation(y_sb[0][:, c0:c1], acc_late[:], COPY)
         for m in range(1, M_TILES):
             acc_y = psum.tile([P, S], F32, name=f"acc_y{m}", tag=("acc_b1", "acc_b2", "acc_h1")[m - 1])
             layer2(acc_y[:], m, 0, S)

@@ -46,11 +46,11 @@ def tile_picked_sub_mlp_silu_sub_e_kernel(tc, xT, w1, w2, gate, offs, pos1, pos2
         w1_grp = [[sb(f"w1_grp{g}_{u}", [P, 2 * H], BF16) for u in range(2)] for g in range(G)]
         w1_words = [sb(f"w1_words{g}", [P, H], U32) for g in range(G)]
         w1_bytes = [sb(f"w1_bytes{g}", [P, H], U8) for g in range(G)]
-        w2_raw = sb("w2_raw", [P, 4, N], F32)
-        w2_cuts = ((0, 128), (128, 256), (256, 512))
-        w2_grp = [sb(f"w2_grp{e}", [P, c1 - c0, 4], BF16) for e, (c0, c1) in enumerate(w2_cuts)]
-        w2_words = [sb("w2_words", [P, P], U32)[:]]
-        w2_bytes = sb("w2_bytes", [P, N], U8)
+        w2_cuts = ((0, N - P), (N - P, N))
+        w2_raw = [sb(f"w2_raw{b}", [P, 4, c1 - c0], F32) for b, (c0, c1) in enumerate(w2_cuts)]
+        w2_grp = [sb(f"w2_grp{m}", [P, P, 4], BF16) for m in range(M_TILES)]
+        w2_words = [sb(f"w2_words{m}", [P, P], U32) for m in range(M_TILES)]
+        w2_bytes = [sb(f"w2_bytes{m}", [P, P], U8) for m in range(M_TILES)]
         h_cuts = ((0, 256), (256, 384), (384, 448), (448, 512))
         h_grp = [sb(f"h_grp{s}", [P, c1 - c0, 4], BF16) for s, (c0, c1) in enumerate(h_cuts)]
         h_bytes = sb("h_bytes", [P, S], U8)
@@ -69,9 +69,10 @@ def tile_picked_sub_mlp_silu_sub_e_kernel(tc, xT, w1, w2, gate, offs, pos1, pos2
                 nc.sync.dma_start(offs_sb[:], offs)
         for g in range(G):
             nc.sync.dma_start(out=w1_raw[g][:], in_=w1[512 * g : 512 * (g + 1), :].rearrange("(p j) c -> p j c", j=4))
-        w2_rows = w2.rearrange("(a u i e) c -> i a u (e c)", u=2, i=2, e=2)
-        for i in range(2):
-            nc.sync.dma_start(out=w2_raw[i:P:2, :, :].rearrange("p (u e) c -> p u (e c)", u=2), in_=w2_rows[i])
+        w2_rows = w2.rearrange("(a j i) c -> i a j c", j=4, i=2)
+        for b, (c0, c1) in enumerate(w2_cuts):
+            for i in range(2):
+                nc.sync.dma_start(out=w2_raw[b][i:P:2, :, :], in_=w2_rows[i, :, :, c0:c1])
         for d, pos in enumerate((pos1, pos2, pos3, pos4)):
             nc.sync.dma_start(pos_sb[d][:], pos)
         nc.sync.dma_start(out=gates[:], in_=gate[:, 0:P, :].rearrange("d p v -> p d v"))
@@ -98,8 +99,8 @@ def tile_picked_sub_mlp_silu_sub_e_kernel(tc, xT, w1, w2, gate, offs, pos1, pos2
             )
 
         def cast_w1(g, engine, u, a0, a1):
-            src = w1_raw[g][:].rearrange("p j (a u i e) -> p u a j i e", u=2, i=2, e=2)[:, u, a0:a1]
-            dst = w1_grp[g][u][:].rearrange("p (e a i j) -> p a j i e", e=2, i=2, j=4)[:, a0:a1]
+            src = w1_raw[g][:].rearrange("p j (a u e i) -> p u a j e i", u=2, i=2, e=2)[:, u, a0:a1]
+            dst = w1_grp[g][u][:].rearrange("p (e a i j) -> p a j e i", e=2, i=2, j=4)[:, a0:a1]
             if engine == "v":
                 nc.vector.tensor_copy(dst, src)
             else:
@@ -167,34 +168,34 @@ def tile_picked_sub_mlp_silu_sub_e_kernel(tc, xT, w1, w2, gate, offs, pos1, pos2
                 for t in (3, 2, 1, 0):
                     layer1(acc_h[s][:, t, :], t, P * s, P * (s + 1), g, False, g == left[-1] and t == 0)
 
-        def cast_w2(part):
-            c0, c1 = w2_cuts[part]
+        def cast_w2(m):
+            b = m // (M_TILES - 1)
+            c0 = P * m - w2_cuts[b][0]
             nc.vector.tensor_copy(
-                w2_grp[part][:].rearrange("p (c i) j -> p c j i", i=4),
-                w2_raw[:, :, c0:c1].rearrange("p j (c i) -> p c j i", i=4),
+                w2_grp[m][:].rearrange("p (c i) j -> p c j i", i=4),
+                w2_raw[b][:, :, c0 : c0 + P].rearrange("p j (c i) -> p c j i", i=4),
             )
 
-        def quant_w2(part, words):
-            c0, c1 = w2_cuts[part]
+        def quant_w2(m):
             nc.vector.quantize_mx(
-                out=words.bitcast(FP8X4),
-                scales=w2_bytes[:, c0:c1],
-                in_=w2_grp[part][:].rearrange("p c j -> p (c j)"),
+                out=w2_words[m][:].bitcast(FP8X4),
+                scales=w2_bytes[m][:],
+                in_=w2_grp[m][:].rearrange("p c j -> p (c j)"),
             )
 
-        cast_w2(0)
-        cast_w2(1)
-        quant_w2(0, w2_words[0])
-        cast_w2(2)
-        h_words = sb("h_words", [P, S], U32, tag="w2_grp0")
+        for m in range(M_TILES - 1):
+            cast_w2(m)
+        quant_w2(0)
+        quant_w2(1)
+        h_words = sb("h_words", [P, S], U32, tag="w2_raw0")
 
         acc_y0 = psum.tile([P, 2 * P], F32, name="acc_y0")
 
         def layer2(dst, m, c0, c1):
             nc.tensor.matmul_mx(
                 out=dst,
-                lhsT=w2_words[m].bitcast(FP8X4),
-                lhsT_scale=w2_bytes[:, P * m : P * (m + 1)],
+                lhsT=w2_words[m][:].bitcast(FP8X4),
+                lhsT_scale=w2_bytes[m][:],
                 rhs=h_words[:, c0:c1].bitcast(FP8X4),
                 rhs_scale=h_bytes[:, c0:c1],
                 start=True,
@@ -217,10 +218,9 @@ def tile_picked_sub_mlp_silu_sub_e_kernel(tc, xT, w1, w2, gate, offs, pos1, pos2
             quant_h(h_grp[s], c0, c1)
             if s == 0:
                 layer2(acc_y0[:], 0, c0, c1)
-        w2_late = sb("w2_late", [P, N - P], U32, tag=f"h_grp{len(h_cuts) - 1}")
-        w2_words.extend(w2_late[:, P * m : P * (m + 1)] for m in range(M_TILES - 1))
-        quant_w2(1, w2_late[:, :P])
-        quant_w2(2, w2_late[:, P:])
+        cast_w2(M_TILES - 1)
+        quant_w2(2)
+        quant_w2(3)
         nc.scalar.activation(y_sb[0][:, : 2 * P], acc_y0[:], COPY)
         for (c0, c1), tag in zip(h_cuts[1:], ("acc_h0", "acc_b0", "acc_h1")):
             acc_late = psum.tile([P, c1 - c0], F32, name=f"acc_late{c0}", tag=tag)

@@ -226,68 +226,99 @@ def tile_picked_sub_mlp_silu_sub_e_kernel(tc, xT, w1, w2, gate, offs, pos1, pos2
             acc_late = psum.tile([P, c1 - c0], F32, name=f"acc_late{c0}", tag=tag)
             layer2(acc_late[:], 0, c0, c1)
             nc.scalar.activation(y_sb[0][:, c0:c1], acc_late[:], COPY)
+        acc_y = {m: psum.tile([P, S], F32, name=f"acc_y{m}", tag=("acc_b1", "acc_b2", "acc_h1")[m - 1]) for m in range(1, M_TILES)}
         for m in range(1, M_TILES):
-            acc_y = psum.tile([P, S], F32, name=f"acc_y{m}", tag=("acc_b1", "acc_b2", "acc_h1")[m - 1])
-            layer2(acc_y[:], m, 0, S)
-            nc.scalar.activation(y_sb[m][:], acc_y[:], COPY)
+            layer2(acc_y[m][:], m, 0, S)
 
-        last_tile = M_TILES - 1
-        sum_tags = ("acc_h2", "acc_h3", "acc_y0")
-        back_tags = ("acc_b0", "acc_b1", "acc_b2")
-        acc_t = [psum.tile([P, V], F32, name=f"acc_t{m}", tag=sum_tags[m]) for m in range(last_tile)]
-        acc_o = [psum.tile([P, V], F32, name=f"acc_o{m}", tag=back_tags[m]) for m in range(last_tile)]
+        sum_tags = ("acc_h2", "acc_h3", "acc_y0", "acc_h0")
+        back_tags = ("acc_b0", "acc_b1", "acc_b2", "acc_h1")
+        acc_t = {}
+        acc_o = {}
+        plain = [sb(f"plain{m}", [P, D, V], F32) for m in range(M_TILES)]
+        slot = {(m, d): terms[m][:, d, :] for m in range(M_TILES) for d in range(D)}
+        for early, late in (((0, 3), (2, 1)), ((0, 2), (3, 0)), ((1, 1), (3, 1)), ((1, 0), (2, 3)), ((1, 3), (3, 3))):
+            slot[early] = plain[late[0]][:, late[1], :]
+        turns = [0] * M_TILES
+        through = (D, D, D - 1, D - 1)
 
-        def fetch(m, d, u0=0, u1=V // P):
-            nc.vector.tensor_tensor(
-                terms[m][:, d, P * u0 : P * u1],
-                y_sb[m][:].indirect(pos_sb[d][:, 8 * u0 : 8 * u1]),
-                gates[:, d, P * u0 : P * u1],
-                MULT,
-            )
+        def leave(m):
+            nc.scalar.activation(y_sb[m][:], acc_y[m][:], COPY)
 
-        def turn_and_add(dst, m, d, u, start, stop):
-            nc.tensor.matmul(
-                dst,
-                lhsT=terms[m][:, d, P * u : P * (u + 1)],
-                rhs=ident[:],
-                start=start,
-                stop=stop,
-                is_transpose=True,
-            )
+        def turn_and_add(m, d):
+            if turns[m] == 0:
+                acc_t[m] = psum.tile([P, V], F32, name=f"acc_t{m}", tag=sum_tags[m])
+            for u in range(V // P):
+                nc.tensor.matmul(
+                    acc_t[m][:, P * u : P * (u + 1)],
+                    lhsT=slot[m, d][:, P * u : P * (u + 1)],
+                    rhs=ident[:],
+                    start=turns[m] == 0 and u == 0,
+                    stop=turns[m] == through[m] - 1 and u == V // P - 1,
+                    is_transpose=True,
+                )
+            turns[m] = turns[m] + 1
 
-        def store(m, c0, c1):
-            nc.sync.dma_start(out=out[P * m : P * (m + 1), c0:c1], in_=sums[m][:, c0:c1])
+        def fetch(m, d):
+            nc.vector.tensor_tensor(slot[m, d], y_sb[m][:].indirect(pos_sb[d][:]), gates[:, d, :], MULT)
+            turn_and_add(m, d)
 
-        for m in range(last_tile):
-            last = D - 1 if m < last_tile - 1 else D - 2
-            for d in range(last + 1):
-                fetch(m, d)
-                for u in range(V // P):
-                    turn_and_add(acc_t[m][:, P * u : P * (u + 1)], m, d, u, d == 0 and u == 0, d == last and u == V // P - 1)
+        def pick(m, d):
+            nc.scalar.activation(plain[m][:, d, :], y_sb[m][:].indirect(pos_sb[d][:]), COPY)
+
+        def weigh(m, d0, d1, turn=True):
+            dst = slot[m, d0] if d1 - d0 == 1 else terms[m][:, d0:d1, :]
+            src = plain[m][:, d0, :] if d1 - d0 == 1 else plain[m][:, d0:d1, :]
+            nc.vector.tensor_tensor(dst, src, gates[:, d0, :] if d1 - d0 == 1 else gates[:, d0:d1, :], MULT)
+            if turn:
+                for d in range(d0, d1):
+                    turn_and_add(m, d)
+
+        def turn_back(m):
             nc.scalar.activation(turned[m][:], acc_t[m][:], COPY)
+            acc_o[m] = psum.tile([P, V], F32, name=f"acc_o{m}", tag=back_tags[m])
             for u in range(V // P):
                 nc.tensor.transpose(acc_o[m][:, P * u : P * (u + 1)], turned[m][:, P * u : P * (u + 1)], ident[:])
-            if last == D - 1:
-                nc.scalar.activation(sums[m][:], acc_o[m][:], COPY)
-                store(m, 0, V)
 
-        m = last_tile
-        half_t = [psum.tile([P, P], F32, name=f"half_t{u}", tag=("acc_h0", "acc_h2")[u]) for u in range(V // P)]
-        half_o = [psum.tile([P, P], F32, name=f"half_o{u}", tag=("acc_h1", "acc_b0")[u]) for u in range(V // P)]
-        for d in range(D - 2):
-            fetch(m, d)
-            for u in range(V // P):
-                turn_and_add(half_t[u][:], m, d, u, d == 0, False)
-        for u in range(V // P):
-            fetch(m, D - 2, u, u + 1)
-            turn_and_add(half_t[u][:], m, D - 2, u, False, True)
-            nc.scalar.activation(turned[m][:, P * u : P * (u + 1)], half_t[u][:], COPY)
-            nc.tensor.transpose(half_o[u][:], turned[m][:, P * u : P * (u + 1)], ident[:])
-        fetch(m - 1, D - 1)
-        fetch(m, D - 1)
-        nc.vector.tensor_tensor(sums[m - 1][:], acc_o[m - 1][:], terms[m - 1][:, D - 1, :], ADD)
-        store(m - 1, 0, V)
-        for u in range(V // P):
-            cols = slice(P * u, P * (u + 1))
-            nc.vector.tensor_tensor(sums[m][:, cols], half_o[u][:], terms[m][:, D - 1, cols], ADD)
-            store(m, P * u, P * (u + 1))
+        def store(m):
+            nc.sync.dma_start(out=out[P * m : P * (m + 1), :], in_=sums[m][:])
+
+        def finish_copy(m):
+            nc.scalar.activation(sums[m][:], acc_o[m][:], COPY)
+            store(m)
+
+        def finish_add(m):
+            nc.vector.tensor_tensor(sums[m][:], acc_o[m][:], terms[m][:, D - 1, :], ADD)
+            store(m)
+
+        leave(1)
+        fetch(0, 0)
+        leave(2)
+        fetch(0, 1)
+        pick(1, 0)
+        fetch(0, 2)
+        pick(2, 0)
+        fetch(0, 3)
+        leave(3)
+        pick(3, 0)
+        turn_back(0)
+        fetch(1, 1)
+        pick(2, 1)
+        fetch(1, 2)
+        finish_copy(0)
+        fetch(1, 3)
+        weigh(1, 0, 1)
+        pick(3, 1)
+        weigh(2, 0, 2)
+        turn_back(1)
+        weigh(3, 0, 2)
+        pick(2, 3)
+        fetch(2, 2)
+        pick(3, 3)
+        fetch(3, 2)
+        turn_back(2)
+        finish_copy(1)
+        weigh(2, 3, 4, False)
+        turn_back(3)
+        weigh(3, 3, 4, False)
+        finish_add(2)
+        finish_add(3)

@@ -230,37 +230,54 @@ def tile_picked_sub_mlp_silu_sub_e_kernel(tc, xT, w1, w2, gate, offs, pos1, pos2
         for m in range(1, M_TILES):
             layer2(acc_y[m][:], m, 0, S)
 
-        sum_tags = ("acc_h2", "acc_h3", "acc_y0", "acc_h0")
-        back_tags = ("acc_b0", "acc_b1", "acc_b2", "acc_h1")
+        halves = V // P
+        last_tile = M_TILES - 1
+        sum_tags = {(0, 0): "acc_h2", (1, 0): "acc_h3", (2, 0): "acc_y0", (3, 0): "acc_h0", (3, 1): "acc_h2"}
+        back_tags = {(0, 0): "acc_b0", (1, 0): "acc_b1", (2, 0): "acc_b2", (3, 0): "acc_h1", (3, 1): "acc_b0"}
         acc_t = {}
         acc_o = {}
         plain = [sb(f"plain{m}", [P, D, V], F32) for m in range(M_TILES)]
         slot = {(m, d): terms[m][:, d, :] for m in range(M_TILES) for d in range(D)}
-        for early, late in (((0, 3), (2, 1)), ((0, 2), (3, 0)), ((1, 1), (3, 1)), ((1, 0), (2, 3)), ((1, 3), (3, 3))):
+        for early, late in (((0, 3), (2, 1)), ((1, 3), (3, 0))):
             slot[early] = plain[late[0]][:, late[1], :]
-        turns = [0] * M_TILES
+        turns = {(m, u): 0 for m in range(M_TILES) for u in range(halves)}
         through = (D, D, D - 1, D - 1)
+
+        def region(banks, tags, kind, m, u):
+            key = (m, u if m == last_tile else 0)
+            if key not in banks:
+                banks[key] = psum.tile([P, P if m == last_tile else V], F32, name=f"{kind}{m}_{key[1]}", tag=tags[key])
+            return banks[key][:] if m == last_tile else banks[key][:, P * u : P * (u + 1)]
 
         def leave(m):
             nc.scalar.activation(y_sb[m][:], acc_y[m][:], COPY)
 
-        def turn_and_add(m, d):
-            if turns[m] == 0:
-                acc_t[m] = psum.tile([P, V], F32, name=f"acc_t{m}", tag=sum_tags[m])
-            for u in range(V // P):
+        def turn_and_add(m, d, u0=0, u1=halves):
+            for u in range(u0, u1):
+                first = turns[m, u] == 0 and (u == 0 or m == last_tile)
+                last = turns[m, u] == through[m] - 1 and (u == halves - 1 or m == last_tile)
                 nc.tensor.matmul(
-                    acc_t[m][:, P * u : P * (u + 1)],
+                    region(acc_t, sum_tags, "acc_t", m, u),
                     lhsT=slot[m, d][:, P * u : P * (u + 1)],
                     rhs=ident[:],
-                    start=turns[m] == 0 and u == 0,
-                    stop=turns[m] == through[m] - 1 and u == V // P - 1,
+                    start=first,
+                    stop=last,
                     is_transpose=True,
                 )
-            turns[m] = turns[m] + 1
+                turns[m, u] = turns[m, u] + 1
 
-        def fetch(m, d):
-            nc.vector.tensor_tensor(slot[m, d], y_sb[m][:].indirect(pos_sb[d][:]), gates[:, d, :], MULT)
-            turn_and_add(m, d)
+        def fetch(m, d, u0=0, u1=halves, turn=True):
+            nc.vector.tensor_tensor(
+                slot[m, d][:, P * u0 : P * u1],
+                y_sb[m][:].indirect(pos_sb[d][:, 8 * u0 : 8 * u1]),
+                gates[:, d, P * u0 : P * u1],
+                MULT,
+            )
+            if turn:
+                turn_and_add(m, d, u0, u1)
+
+        def keep_term(m):
+            fetch(m, D - 1, turn=False)
 
         def pick(m, d):
             nc.scalar.activation(plain[m][:, d, :], y_sb[m][:].indirect(pos_sb[d][:]), COPY)
@@ -273,52 +290,54 @@ def tile_picked_sub_mlp_silu_sub_e_kernel(tc, xT, w1, w2, gate, offs, pos1, pos2
                 for d in range(d0, d1):
                     turn_and_add(m, d)
 
-        def turn_back(m):
-            nc.scalar.activation(turned[m][:], acc_t[m][:], COPY)
-            acc_o[m] = psum.tile([P, V], F32, name=f"acc_o{m}", tag=back_tags[m])
-            for u in range(V // P):
-                nc.tensor.transpose(acc_o[m][:, P * u : P * (u + 1)], turned[m][:, P * u : P * (u + 1)], ident[:])
+        def turn_back(m, u0=0, u1=halves):
+            src = acc_t[m, u0][:] if m == last_tile else acc_t[m, 0][:]
+            nc.scalar.activation(turned[m][:, P * u0 : P * u1], src, COPY)
+            for u in range(u0, u1):
+                nc.tensor.transpose(region(acc_o, back_tags, "acc_o", m, u), turned[m][:, P * u : P * (u + 1)], ident[:])
 
-        def store(m):
-            nc.sync.dma_start(out=out[P * m : P * (m + 1), :], in_=sums[m][:])
+        def store(m, u0=0, u1=halves):
+            nc.sync.dma_start(out=out[P * m : P * (m + 1), P * u0 : P * u1], in_=sums[m][:, P * u0 : P * u1])
 
         def finish_copy(m):
-            nc.scalar.activation(sums[m][:], acc_o[m][:], COPY)
+            nc.scalar.activation(sums[m][:], acc_o[m, 0][:], COPY)
             store(m)
 
-        def finish_add(m):
-            nc.vector.tensor_tensor(sums[m][:], acc_o[m][:], terms[m][:, D - 1, :], ADD)
-            store(m)
+        def finish_add(m, u0=0, u1=halves):
+            cols = slice(P * u0, P * u1)
+            nc.vector.tensor_tensor(sums[m][:, cols], acc_o[m, u0][:], slot[m, D - 1][:, cols], ADD)
+            store(m, u0, u1)
 
         leave(1)
         fetch(0, 0)
-        leave(2)
-        fetch(0, 1)
         pick(1, 0)
+        fetch(0, 1)
+        leave(2)
         fetch(0, 2)
-        pick(2, 0)
+        pick(1, 1)
         fetch(0, 3)
-        leave(3)
-        pick(3, 0)
-        turn_back(0)
-        fetch(1, 1)
-        pick(2, 1)
+        pick(2, 0)
         fetch(1, 2)
-        finish_copy(0)
+        turn_back(0)
         fetch(1, 3)
-        weigh(1, 0, 1)
-        pick(3, 1)
+        pick(2, 1)
+        weigh(1, 0, 2)
+        leave(3)
+        fetch(2, 2)
+        finish_copy(0)
+        pick(3, 0)
         weigh(2, 0, 2)
         turn_back(1)
-        weigh(3, 0, 2)
-        pick(2, 3)
-        fetch(2, 2)
-        pick(3, 3)
-        fetch(3, 2)
+        fetch(3, 1)
+        weigh(3, 0, 1)
         turn_back(2)
+        fetch(3, 2, 0, 1)
+        turn_back(3, 0, 1)
+        fetch(3, 2, 1, 2)
         finish_copy(1)
-        weigh(2, 3, 4, False)
-        turn_back(3)
-        weigh(3, 3, 4, False)
+        turn_back(3, 1, 2)
+        keep_term(2)
+        keep_term(3)
         finish_add(2)
-        finish_add(3)
+        finish_add(3, 0, 1)
+        finish_add(3, 1, 2)

@@ -55,12 +55,15 @@ def tile_picked_sub_mlp_silu_sub_e_kernel(tc, xT, w1, w2, gate, offs, pos1, pos2
         h_grp = [sb(f"h_grp{s}", [P, c1 - c0, 4], BF16) for s, (c0, c1) in enumerate(h_cuts)]
         h_bytes = sb("h_bytes", [P, S], U8)
         gates = sb("gates", [P, D, V], F32)
+        gate_rows = sb("gate_rows", [P, V], F32)
+        gate_cols = sb("gate_cols", [P, V // P, D], F32)
         y_sb = [sb(f"y_sb{m}", [P, S], F32) for m in range(M_TILES)]
         terms = [sb(f"terms{m}", [P, D, V], F32) for m in range(M_TILES)]
         turned = [sb(f"turned{m}", [P, V], F32) for m in range(M_TILES)]
         ident = sb("ident", [P, P], F32)
         sums = [sb(f"sums{m}", [P, V], F32) for m in range(M_TILES)]
 
+        nc.gpsimd.memset(gate_rows[:], 0.0)
         for g in range(G):
             rows = xT[512 * g : 512 * (g + 1), :].rearrange("(p j) t -> p j t", j=4)
             for e in range(2):
@@ -69,6 +72,7 @@ def tile_picked_sub_mlp_silu_sub_e_kernel(tc, xT, w1, w2, gate, offs, pos1, pos2
                 nc.sync.dma_start(offs_sb[:], offs)
         for g in range(G):
             nc.sync.dma_start(out=w1_raw[g][:], in_=w1[512 * g : 512 * (g + 1), :].rearrange("(p j) c -> p j c", j=4))
+        nc.sync.dma_start(out=gate_rows[0:D, :], in_=gate[:, P, :])
         w2_rows = w2.rearrange("(a j i) c -> i a j c", j=4, i=2)
         for b, (c0, c1) in enumerate(w2_cuts):
             for i in range(2):
@@ -168,6 +172,11 @@ def tile_picked_sub_mlp_silu_sub_e_kernel(tc, xT, w1, w2, gate, offs, pos1, pos2
                 for t in (3, 2, 1, 0):
                     layer1(acc_h[s][:, t, :], t, P * s, P * (s + 1), g, False, g == left[-1] and t == 0)
 
+        acc_g = psum.tile([P, V // P, P], F32, name="acc_g", tag="acc_b0")
+        for u in range(V // P):
+            nc.tensor.transpose(acc_g[:, u, :], gate_rows[:, P * u : P * (u + 1)], ident[:])
+        nc.scalar.activation(gate_cols[:], acc_g[:, :, 0:D], COPY)
+
         def cast_w2(m):
             b = m // (M_TILES - 1)
             c0 = P * m - w2_cuts[b][0]
@@ -232,14 +241,23 @@ def tile_picked_sub_mlp_silu_sub_e_kernel(tc, xT, w1, w2, gate, offs, pos1, pos2
 
         halves = V // P
         last_tile = M_TILES - 1
-        sum_tags = {(0, 0): "acc_h2", (1, 0): "acc_h3", (2, 0): "acc_y0", (3, 0): "acc_h0", (3, 1): "acc_h2"}
-        back_tags = {(0, 0): "acc_b0", (1, 0): "acc_b1", (2, 0): "acc_b2", (3, 0): "acc_h1", (3, 1): "acc_b0"}
+        sum_tags = {(0, 0): "acc_h2", (1, 0): "acc_h3", (2, 0): "acc_y0", (3, 0): "acc_h1", (3, 1): "acc_h3"}
+        back_tags = {(0, 0): "acc_b0", (1, 0): "acc_b1", (2, 0): "acc_b0", (3, 0): "acc_h0", (3, 1): "acc_b2"}
+        pick_tags = ("acc_h3", "acc_h0", "acc_b2", "acc_h2")
+        acc_p = {}
         acc_t = {}
         acc_o = {}
-        plain = [sb(f"plain{m}", [P, D, V], F32) for m in range(M_TILES)]
+        scaled = [sb(f"scaled{d}", [P, V], F32) for d in range(D)]
         slot = {(m, d): terms[m][:, d, :] for m in range(M_TILES) for d in range(D)}
-        for early, late in (((0, 3), (2, 1)), ((1, 3), (3, 0))):
-            slot[early] = plain[late[0]][:, late[1], :]
+        slot[1, 0] = slot[0, 0]
+        slot[1, 1] = slot[0, 1]
+        slot[1, 2] = slot[0, 2]
+        slot[1, 3] = slot[2, 0]
+        slot[3, 0] = slot[1, 0]
+        slot[3, 1] = slot[1, 1]
+        slot[3, 2] = turned[0][:]
+        slot[2, 3] = scaled[0][:]
+        slot[3, 3] = slot[1, 3]
         turns = {(m, u): 0 for m in range(M_TILES) for u in range(halves)}
         through = (D, D, D - 1, D - 1)
 
@@ -280,15 +298,24 @@ def tile_picked_sub_mlp_silu_sub_e_kernel(tc, xT, w1, w2, gate, offs, pos1, pos2
             fetch(m, D - 1, turn=False)
 
         def pick(m, d):
-            nc.scalar.activation(plain[m][:, d, :], y_sb[m][:].indirect(pos_sb[d][:]), COPY)
+            nc.scalar.activation(slot[m, d], y_sb[m][:].indirect(pos_sb[d][:]), COPY)
+            acc_p[d] = psum.tile([P, V], F32, name=f"acc_p{d}", tag=pick_tags[d])
+            for u in range(halves):
+                nc.tensor.transpose(acc_p[d][:, P * u : P * (u + 1)], slot[m, d][:, P * u : P * (u + 1)], ident[:])
 
-        def weigh(m, d0, d1, turn=True):
-            dst = slot[m, d0] if d1 - d0 == 1 else terms[m][:, d0:d1, :]
-            src = plain[m][:, d0, :] if d1 - d0 == 1 else plain[m][:, d0:d1, :]
-            nc.vector.tensor_tensor(dst, src, gates[:, d0, :] if d1 - d0 == 1 else gates[:, d0:d1, :], MULT)
-            if turn:
-                for d in range(d0, d1):
-                    turn_and_add(m, d)
+        def scale_back(m, d):
+            for u in range(halves):
+                cols = slice(P * u, P * (u + 1))
+                nc.scalar.activation(scaled[d][:, cols], acc_p[d][:, cols], COPY, scale=gate_cols[:, u, d : d + 1])
+            for u in range(halves):
+                nc.tensor.matmul(
+                    region(acc_o, back_tags, "acc_o", m, u),
+                    lhsT=scaled[d][:, P * u : P * (u + 1)],
+                    rhs=ident[:],
+                    start=d == 0 and u == 0,
+                    stop=d == D - 1 and u == halves - 1,
+                    is_transpose=True,
+                )
 
         def turn_back(m, u0=0, u1=halves):
             src = acc_t[m, u0][:] if m == last_tile else acc_t[m, 0][:]
@@ -310,34 +337,34 @@ def tile_picked_sub_mlp_silu_sub_e_kernel(tc, xT, w1, w2, gate, offs, pos1, pos2
 
         leave(1)
         fetch(0, 0)
-        pick(1, 0)
-        fetch(0, 1)
         leave(2)
-        fetch(0, 2)
-        pick(1, 1)
-        fetch(0, 3)
-        pick(2, 0)
-        fetch(1, 2)
-        turn_back(0)
-        fetch(1, 3)
-        pick(2, 1)
-        weigh(1, 0, 2)
+        fetch(0, 1)
         leave(3)
+        fetch(0, 2)
+        pick(1, 0)
+        fetch(0, 3)
+        pick(1, 1)
+        fetch(2, 0)
+        pick(1, 2)
+        fetch(2, 1)
+        turn_back(0)
         fetch(2, 2)
-        finish_copy(0)
-        pick(3, 0)
-        weigh(2, 0, 2)
-        turn_back(1)
+        scale_back(1, 0)
+        fetch(3, 0)
+        pick(1, 3)
+        scale_back(1, 1)
         fetch(3, 1)
-        weigh(3, 0, 1)
-        turn_back(2)
+        finish_copy(0)
         fetch(3, 2, 0, 1)
-        turn_back(3, 0, 1)
         fetch(3, 2, 1, 2)
-        finish_copy(1)
-        turn_back(3, 1, 2)
+        scale_back(1, 2)
+        turn_back(2)
         keep_term(2)
+        scale_back(1, 3)
+        turn_back(3, 0, 1)
+        turn_back(3, 1, 2)
         keep_term(3)
+        finish_copy(1)
         finish_add(2)
         finish_add(3, 0, 1)
         finish_add(3, 1, 2)

@@ -56,7 +56,6 @@ def tile_picked_sub_mlp_silu_sub_e_kernel(tc, xT, w1, w2, gate, offs, pos1, pos2
         h_bytes = sb("h_bytes", [P, S], U8)
         gates = sb("gates", [P, D, V], F32)
         gate_rows = sb("gate_rows", [P, V], F32)
-        gate_cols = sb("gate_cols", [P, V // P, D], F32)
         y_sb = [sb(f"y_sb{m}", [P, S], F32) for m in range(M_TILES)]
         terms = [sb(f"terms{m}", [P, D, V], F32) for m in range(M_TILES)]
         turned = [sb(f"turned{m}", [P, V], F32) for m in range(M_TILES)]
@@ -172,11 +171,6 @@ def tile_picked_sub_mlp_silu_sub_e_kernel(tc, xT, w1, w2, gate, offs, pos1, pos2
                 for t in (3, 2, 1, 0):
                     layer1(acc_h[s][:, t, :], t, P * s, P * (s + 1), g, False, g == left[-1] and t == 0)
 
-        acc_g = psum.tile([P, V // P, P], F32, name="acc_g", tag="acc_b0")
-        for u in range(V // P):
-            nc.tensor.transpose(acc_g[:, u, :], gate_rows[:, P * u : P * (u + 1)], ident[:])
-        nc.scalar.activation(gate_cols[:], acc_g[:, :, 0:D], COPY)
-
         def cast_w2(m):
             b = m // (M_TILES - 1)
             c0 = P * m - w2_cuts[b][0]
@@ -249,7 +243,10 @@ def tile_picked_sub_mlp_silu_sub_e_kernel(tc, xT, w1, w2, gate, offs, pos1, pos2
         acc_o = {}
         scaled = [sb(f"scaled{d}", [P, V], F32) for d in range(D)]
         slot = {(m, d): terms[m][:, d, :] for m in range(M_TILES) for d in range(D)}
-        slot[1, 0] = slot[0, 0]
+        first = sb("first", [P, 3 * P], F32)
+        gate_cols = first[:, 0 : halves * D].rearrange("p (u d) -> p u d", d=D)
+        slot[0, 0] = first[:, 0:V]
+        slot[1, 0] = first[:, P : P + V]
         slot[1, 1] = slot[0, 1]
         slot[1, 2] = slot[0, 2]
         slot[1, 3] = slot[2, 0]
@@ -323,6 +320,17 @@ def tile_picked_sub_mlp_silu_sub_e_kernel(tc, xT, w1, w2, gate, offs, pos1, pos2
             for u in range(u0, u1):
                 nc.tensor.transpose(region(acc_o, back_tags, "acc_o", m, u), turned[m][:, P * u : P * (u + 1)], ident[:])
 
+        def keep_clock(tag):
+            idle = psum.tile([P, S], F32, name=f"idle_{tag}", tag=tag)
+            for m in range(2):
+                layer2(idle[:], m, 0, S)
+
+        def turn_gate():
+            acc_g = psum.tile([P, halves, P], F32, name="acc_g", tag="acc_b1")
+            for u in range(halves):
+                nc.tensor.transpose(acc_g[:, u, :], gate_rows[:, P * u : P * (u + 1)], ident[:])
+            nc.scalar.activation(gate_cols, acc_g[:, :, 0:D], COPY)
+
         def store(m, u0=0, u1=halves):
             nc.sync.dma_start(out=out[P * m : P * (m + 1), P * u0 : P * u1], in_=sums[m][:, P * u0 : P * u1])
 
@@ -340,6 +348,8 @@ def tile_picked_sub_mlp_silu_sub_e_kernel(tc, xT, w1, w2, gate, offs, pos1, pos2
         leave(2)
         fetch(0, 1)
         leave(3)
+        turn_gate()
+        keep_clock("acc_b1")
         fetch(0, 2)
         pick(1, 0)
         fetch(0, 3)
@@ -348,6 +358,7 @@ def tile_picked_sub_mlp_silu_sub_e_kernel(tc, xT, w1, w2, gate, offs, pos1, pos2
         pick(1, 2)
         fetch(2, 1)
         turn_back(0)
+        keep_clock("acc_h2")
         fetch(2, 2)
         scale_back(1, 0)
         fetch(3, 0)

@@ -56,7 +56,7 @@ def tile_picked_sub_mlp_silu_sub_e_kernel(tc, xT, w1, w2, gate, offs, pos1, pos2
         h_bytes = sb("h_bytes", [P, S], U8)
         gates = sb("gates", [P, D, V], F32)
         gate_rows = sb("gate_rows", [P, V], F32)
-        y_sb = [sb(f"y_sb{m}", [P, S], F32) for m in range(M_TILES)]
+        y_sb = {m: sb(f"y_sb{m}", [P, S], F32) for m in range(M_TILES) if m != 1}
         terms = [sb(f"terms{m}", [P, D, V], F32) for m in range(M_TILES)]
         turned = [sb(f"turned{m}", [P, V], F32) for m in range(M_TILES)]
         ident = sb("ident", [P, P], F32)
@@ -190,6 +190,7 @@ def tile_picked_sub_mlp_silu_sub_e_kernel(tc, xT, w1, w2, gate, offs, pos1, pos2
             cast_w2(m)
         quant_w2(0)
         quant_w2(1)
+        quant_w2(2)
         h_words = sb("h_words", [P, S], U32, tag="w2_raw0")
 
         acc_y0 = psum.tile([P, 2 * P], F32, name="acc_y0")
@@ -221,23 +222,31 @@ def tile_picked_sub_mlp_silu_sub_e_kernel(tc, xT, w1, w2, gate, offs, pos1, pos2
             quant_h(h_grp[s], c0, c1)
             if s == 0:
                 layer2(acc_y0[:], 0, c0, c1)
+                acc_y1 = psum.tile([P, 2 * P], F32, name="acc_y1_early", tag="acc_h2")
+                layer2(acc_y1[:], 1, c0, c1)
+                acc_y2 = psum.tile([P, S], F32, name="acc_y2", tag="acc_b2")
+                layer2(acc_y2[:, c0:c1], 2, c0, c1)
         cast_w2(M_TILES - 1)
-        quant_w2(2)
         quant_w2(3)
+        y_sb[1] = sb("y_sb1", [P, S], F32, tag=f"h_grp{len(h_cuts) - 1}")
+        nc.vector.tensor_copy(y_sb[1][:, : 2 * P], acc_y1[:])
         nc.scalar.activation(y_sb[0][:, : 2 * P], acc_y0[:], COPY)
         for (c0, c1), tag in zip(h_cuts[1:], ("acc_h0", "acc_b0", "acc_h1")):
             acc_late = psum.tile([P, c1 - c0], F32, name=f"acc_late{c0}", tag=tag)
             layer2(acc_late[:], 0, c0, c1)
             nc.scalar.activation(y_sb[0][:, c0:c1], acc_late[:], COPY)
-        acc_y = {m: psum.tile([P, S], F32, name=f"acc_y{m}", tag=("acc_b1", "acc_b2", "acc_h1")[m - 1]) for m in range(1, M_TILES)}
-        for m in range(1, M_TILES):
-            layer2(acc_y[m][:], m, 0, S)
+        y_from = {1: 2 * P, 2: 0, 3: 0}
+        acc_y = {m: psum.tile([P, S - y_from[m]], F32, name=f"acc_y{m}", tag=tag) for m, tag in ((1, "acc_b1"), (3, "acc_h1"))}
+        acc_y[2] = acc_y2
+        layer2(acc_y[1][:], 1, 2 * P, S)
+        layer2(acc_y[2][:, 2 * P :], 2, 2 * P, S)
+        layer2(acc_y[3][:], 3, 0, S)
 
         halves = V // P
         last_tile = M_TILES - 1
-        sum_tags = {(0, 0): "acc_h2", (1, 0): "acc_h3", (2, 0): "acc_y0", (3, 0): "acc_h1", (3, 1): "acc_h3"}
+        sum_tags = {(0, 0): "acc_h2", (1, 0): "acc_h3", (2, 0): "acc_y0", (3, 0): "acc_h2", (3, 1): "acc_h3"}
         back_tags = {(0, 0): "acc_b0", (1, 0): "acc_b1", (2, 0): "acc_b0", (3, 0): "acc_h0", (3, 1): "acc_b2"}
-        pick_tags = ("acc_h3", "acc_h0", "acc_b2", "acc_h2")
+        pick_tags = ("acc_h3", "acc_h0", "acc_b2", "acc_h1")
         acc_p = {}
         acc_t = {}
         acc_o = {}
@@ -265,7 +274,7 @@ def tile_picked_sub_mlp_silu_sub_e_kernel(tc, xT, w1, w2, gate, offs, pos1, pos2
             return banks[key][:] if m == last_tile else banks[key][:, P * u : P * (u + 1)]
 
         def leave(m):
-            nc.scalar.activation(y_sb[m][:], acc_y[m][:], COPY)
+            nc.scalar.activation(y_sb[m][:, y_from[m] :], acc_y[m][:], COPY)
 
         def turn_and_add(m, d, u0=0, u1=halves):
             for u in range(u0, u1):
@@ -365,13 +374,13 @@ def tile_picked_sub_mlp_silu_sub_e_kernel(tc, xT, w1, w2, gate, offs, pos1, pos2
         pick(1, 3)
         scale_back(1, 1)
         fetch(3, 1)
-        finish_copy(0)
         fetch(3, 2, 0, 1)
         fetch(3, 2, 1, 2)
         scale_back(1, 2)
-        turn_back(2)
-        keep_term(2)
         scale_back(1, 3)
+        finish_copy(0)
+        keep_term(2)
+        turn_back(2)
         turn_back(3, 0, 1)
         turn_back(3, 1, 2)
         keep_term(3)

@@ -20,8 +20,7 @@ ADD = mybir.AluOpType.add
 P = 128
 G = K // 512
 M_TILES = N // P
-X_SHARE = ((256, 384), (640, 512), (640, 512))
-W1_SHARE = ((64, 64), (42, 42), (0, 48))
+W1_SHARE = ((64, 64), (0, 64), (0, 48))
 
 
 def tile_picked_sub_mlp_silu_sub_e_kernel(tc, xT, w1, w2, gate, offs, pos1, pos2, pos3, pos4, out):
@@ -35,13 +34,13 @@ def tile_picked_sub_mlp_silu_sub_e_kernel(tc, xT, w1, w2, gate, offs, pos1, pos2
 
         offs_sb = sb("offs_sb", [P, S // 16], U16)
         pos_sb = [sb(f"pos_sb{d}", [P, V // 16], U16) for d in range(D)]
-        pieces = 4
-        x_raw = [[sb(f"x_raw{g}_{e}", [P, 2, T], F32) for e in range(2)] for g in range(G)]
-        x_grp = [[sb(f"x_grp{g}_{i}", [P, 256, 4], BF16) for i in range(pieces)] for g in range(G)]
-        x_words = [sb(f"x_words{g}", [P, T], U32) for g in range(G)]
-        x_bytes = sb("x_bytes", [P, T], U8)
-        p_words = [sb(f"p_words{g}", [P, S if g < G - 1 else S // 2], U32) for g in range(G)]
-        p_bytes = sb("p_bytes", [P, S], U8)
+        slices = S // P
+        x_cuts = ((0, 2), (2, 4))
+        x_raw = [[sb(f"x_raw{g}_{j0}", [P, j1 - j0, T], F32) for j0, j1 in x_cuts] for g in range(G)]
+        x_pick = [sb(f"x_pick{g}", [P, 4, S - P], F32) for g in range(G)]
+        x_grp = [sb(f"x_grp{g}", [P, S, 4], BF16) for g in range(G)]
+        p_words = [sb(f"p_words{g}", [P, S], U32) for g in range(G)]
+        p_bytes = [sb(f"p_bytes{g}", [P, S], U8) for g in range(G)]
         w1_raw = [sb(f"w1_raw{g}", [P, 4, H], F32) for g in range(G)]
         w1_grp = [[sb(f"w1_grp{g}_{u}", [P, 2 * H], BF16) for u in range(2)] for g in range(G)]
         w1_words = [sb(f"w1_words{g}", [P, H], U32) for g in range(G)]
@@ -65,10 +64,10 @@ def tile_picked_sub_mlp_silu_sub_e_kernel(tc, xT, w1, w2, gate, offs, pos1, pos2
         nc.gpsimd.memset(gate_rows[:], 0.0)
         for g in range(G):
             rows = xT[512 * g : 512 * (g + 1), :].rearrange("(p j) t -> p j t", j=4)
-            for e in range(2):
-                nc.sync.dma_start(out=x_raw[g][e][:], in_=rows[:, 2 * e : 2 * e + 2, :])
-            if g == 0:
-                nc.sync.dma_start(offs_sb[:], offs)
+            for e, (j0, j1) in enumerate(x_cuts):
+                nc.sync.dma_start(out=x_raw[g][e][:], in_=rows[:, j0:j1, :])
+                if g == 0 and e == 0:
+                    nc.sync.dma_start(offs_sb[:], offs)
         for g in range(G):
             nc.sync.dma_start(out=w1_raw[g][:], in_=w1[512 * g : 512 * (g + 1), :].rearrange("(p j) c -> p j c", j=4))
         nc.sync.dma_start(out=gate_rows[0:D, :], in_=gate[:, P, :])
@@ -80,25 +79,32 @@ def tile_picked_sub_mlp_silu_sub_e_kernel(tc, xT, w1, w2, gate, offs, pos1, pos2
             nc.sync.dma_start(pos_sb[d][:], pos)
         nc.sync.dma_start(out=gates[:], in_=gate[:, 0:P, :].rearrange("d p v -> p d v"))
 
-        nc.gpsimd.memset(x_bytes[:], 0)
         make_identity(nc, ident[:])
         warm = sb("warm", [P, 2], F32)
         nc.vector.memset(warm[:, 0:1], 0.0)
         nc.scalar.activation(warm[:, 1:2], warm[:, 0:1], SILU)
 
-        def cast_x(g, e, i, c0, c1, engine):
-            src = x_raw[g][e][:, :, 256 * i + c0 : 256 * i + c1].rearrange("p j (c i) -> p c j i", i=4)
-            dst = x_grp[g][i][:, c0:c1, 2 * e : 2 * e + 2].rearrange("p (c i) j -> p c j i", i=4)
+        def gather_x(engine, dst, g, j, c0, c1):
+            e = [k for k, (j0, j1) in enumerate(x_cuts) if j0 <= j < j1][0]
+            src = x_raw[g][e][:, j - x_cuts[e][0], :].indirect(offs_sb[:, c0 // 16 : c1 // 16])
             if engine == "v":
                 nc.vector.tensor_copy(dst, src)
             else:
                 nc.scalar.activation(dst, src, COPY)
 
-        def quant_x(g, i):
+        def weave(engine, dst, src):
+            dst = dst.rearrange("p (c i) j -> p c j i", i=4)
+            src = src.rearrange("p j (c i) -> p c j i", i=4)
+            if engine == "v":
+                nc.vector.tensor_copy(dst, src)
+            else:
+                nc.scalar.copy(dst, src)
+
+        def quant_x(grp, g, c0, c1):
             nc.vector.quantize_mx(
-                out=x_words[g][:, 256 * i : 256 * (i + 1)].bitcast(FP8X4),
-                scales=x_bytes[4 * g : P, 256 * i : 256 * (i + 1)],
-                in_=x_grp[g][i][:].rearrange("p c j -> p (c j)"),
+                out=p_words[g][:, c0:c1].bitcast(FP8X4),
+                scales=p_bytes[g][:, c0:c1],
+                in_=grp[:].rearrange("p c j -> p (c j)"),
             )
 
         def cast_w1(g, engine, u, a0, a1):
@@ -113,40 +119,30 @@ def tile_picked_sub_mlp_silu_sub_e_kernel(tc, xT, w1, w2, gate, offs, pos1, pos2
             nc.vector.quantize_mx(
                 out=w1_words[g][:, P * t0 : P * t1].bitcast(FP8X4),
                 scales=w1_bytes[g][:, P * t0 : P * t1],
-                in_=w1_grp[g][t0 // 2][:],
+                in_=w1_grp[g][t0 // 2][:, H * (t0 % 2) : H * (t0 % 2 + t1 - t0)],
             )
 
         for g in range(G):
-            for e in range(2):
-                border = T - X_SHARE[g][e]
-                for i in range(pieces):
-                    cut = min(max(border - 256 * i, 0), 256)
-                    if cut > 0:
-                        cast_x(g, e, i, 0, cut, "v")
-                    if cut < 256:
-                        cast_x(g, e, i, cut, 256, "s")
-            for i in range(pieces):
-                quant_x(g, i)
+            for j in range(4):
+                cut = 2 * P if j >= 2 else P
+                gather_x("v", x_grp[g][:, 0:P, j], g, j, 0, P)
+                if cut > P:
+                    gather_x("v", x_pick[g][:, j, 0 : cut - P], g, j, P, cut)
+                gather_x("s", x_pick[g][:, j, cut - P :], g, j, cut, S)
+            weave("v", x_grp[g][:, P:, :], x_pick[g][:])
             if g < G - 1:
-                nc.vector.tensor_copy(p_words[g][:], x_words[g][:].indirect(offs_sb[:]))
-        nc.vector.tensor_copy(p_bytes[:], x_bytes[:].indirect(offs_sb[:]))
-        nc.vector.tensor_copy(p_words[G - 1][:], x_words[G - 1][:].indirect(offs_sb[:, : S // 32]))
+                quant_x(x_grp[g], g, 0, S)
 
-        slices = S // P
-        late_words = []
         acc_h = [psum.tile([P, 4, P], F32, name=f"acc_h{s}") for s in range(slices)]
 
         def layer1(dst, t, c0, c1, g, start, stop):
-            if g == G - 1 and c0 >= S // 2:
-                words = late_words[0][:, c0 - S // 2 : c1 - S // 2]
-            else:
-                words = p_words[g][:, c0:c1]
+            words = p_words[g][:, c0:c1]
             nc.tensor.matmul_mx(
                 out=dst,
                 lhsT=w1_words[g][:, P * t : P * (t + 1)].bitcast(FP8X4),
                 lhsT_scale=w1_bytes[g][:, P * t : P * (t + 1)],
                 rhs=words.bitcast(FP8X4),
-                rhs_scale=p_bytes[4 * g : P, c0:c1],
+                rhs_scale=p_bytes[g][:, c0:c1],
                 start=start,
                 stop=stop,
             )
@@ -159,12 +155,16 @@ def tile_picked_sub_mlp_silu_sub_e_kernel(tc, xT, w1, w2, gate, offs, pos1, pos2
                 if split < P // 2:
                     cast_w1(g, "v", u, split, P // 2)
             quant_w1(g, 0, 2)
-            quant_w1(g, 2, 4)
+            if g < G - 1:
+                quant_w1(g, 2, 4)
+            else:
+                quant_w1(g, 2, 3)
+                quant_w1(g, 3, 4)
+            if g == 0:
+                quant_x(x_grp[G - 1], G - 1, 0, S)
             for s in range((slices, slices - 1, 1)[g]):
                 for t in range(4):
                     layer1(acc_h[s][:, t, :], t, P * s, P * (s + 1), g, g == 0 and t == 0, g == G - 1 and t == 3)
-        late_words.append(sb("late_words", [P, S // 2], U32, tag=f"w1_grp{G - 1}_1"))
-        nc.vector.tensor_copy(late_words[0][:], x_words[G - 1][:].indirect(offs_sb[:, S // 32 :]))
         for s in range(1, slices):
             left = (2,) if s < slices - 1 else (2, 1)
             for g in left:

@@ -329,11 +329,6 @@ def tile_picked_sub_mlp_silu_sub_e_kernel(tc, xT, w1, w2, gate, offs, pos1, pos2
             for u in range(u0, u1):
                 nc.tensor.transpose(region(acc_o, back_tags, "acc_o", m, u), turned[m][:, P * u : P * (u + 1)], ident[:])
 
-        def keep_clock(tag):
-            idle = psum.tile([P, S], F32, name=f"idle_{tag}", tag=tag)
-            for m in range(2):
-                layer2(idle[:], m, 0, S)
-
         def turn_gate():
             acc_g = psum.tile([P, halves, P], F32, name="acc_g", tag="acc_b1")
             for u in range(halves):
@@ -358,7 +353,6 @@ def tile_picked_sub_mlp_silu_sub_e_kernel(tc, xT, w1, w2, gate, offs, pos1, pos2
         fetch(0, 1)
         leave(3)
         turn_gate()
-        keep_clock("acc_b1")
         fetch(0, 2)
         pick(1, 0)
         fetch(0, 3)
@@ -367,7 +361,6 @@ def tile_picked_sub_mlp_silu_sub_e_kernel(tc, xT, w1, w2, gate, offs, pos1, pos2
         pick(1, 2)
         fetch(2, 1)
         turn_back(0)
-        keep_clock("acc_h2")
         fetch(2, 2)
         scale_back(1, 0)
         fetch(3, 0)

@@ -45,8 +45,7 @@ def tile_picked_sub_mlp_silu_sub_e_kernel(tc, xT, w1, w2, gate, offs, pos1, pos2
         w1_grp = [[sb(f"w1_grp{g}_{u}", [P, 2 * H], BF16) for u in range(2)] for g in range(G)]
         w1_words = [sb(f"w1_words{g}", [P, H], U32) for g in range(G)]
         w1_bytes = [sb(f"w1_bytes{g}", [P, H], U8) for g in range(G)]
-        w2_cuts = ((0, N - P), (N - P, N))
-        w2_raw = [sb(f"w2_raw{b}", [P, 4, c1 - c0], F32) for b, (c0, c1) in enumerate(w2_cuts)]
+        w2_raw = sb("w2_raw", [P, 4, N], F32)
         w2_grp = [sb(f"w2_grp{m}", [P, P, 4], BF16) for m in range(M_TILES)]
         w2_words = [sb(f"w2_words{m}", [P, P], U32) for m in range(M_TILES)]
         w2_bytes = [sb(f"w2_bytes{m}", [P, P], U8) for m in range(M_TILES)]
@@ -55,11 +54,7 @@ def tile_picked_sub_mlp_silu_sub_e_kernel(tc, xT, w1, w2, gate, offs, pos1, pos2
         h_bytes = sb("h_bytes", [P, S], U8)
         gates = sb("gates", [P, D, V], F32)
         gate_rows = sb("gate_rows", [P, V], F32)
-        y_sb = {m: sb(f"y_sb{m}", [P, S], F32) for m in range(M_TILES) if m != 1}
-        terms = [sb(f"terms{m}", [P, D, V], F32) for m in range(M_TILES)]
-        turned = [sb(f"turned{m}", [P, V], F32) for m in range(M_TILES)]
         ident = sb("ident", [P, P], F32)
-        sums = [sb(f"sums{m}", [P, V], F32) for m in range(M_TILES)]
 
         nc.gpsimd.memset(gate_rows[:], 0.0)
         for g in range(G):
@@ -68,13 +63,10 @@ def tile_picked_sub_mlp_silu_sub_e_kernel(tc, xT, w1, w2, gate, offs, pos1, pos2
                 nc.sync.dma_start(out=x_raw[g][e][:], in_=rows[:, j0:j1, :])
                 if g == 0 and e == 0:
                     nc.sync.dma_start(offs_sb[:], offs)
+                    nc.sync.dma_start(out=gate_rows[0:D, :], in_=gate[:, P, :])
         for g in range(G):
             nc.sync.dma_start(out=w1_raw[g][:], in_=w1[512 * g : 512 * (g + 1), :].rearrange("(p j) c -> p j c", j=4))
-        nc.sync.dma_start(out=gate_rows[0:D, :], in_=gate[:, P, :])
-        w2_rows = w2.rearrange("(a j i) c -> i a j c", j=4, i=2)
-        for b, (c0, c1) in enumerate(w2_cuts):
-            for i in range(2):
-                nc.sync.dma_start(out=w2_raw[b][i:P:2, :, :], in_=w2_rows[i, :, :, c0:c1])
+        nc.sync.dma_start(out=w2_raw[:], in_=w2.rearrange("(p j) c -> p j c", j=4))
         for d, pos in enumerate((pos1, pos2, pos3, pos4)):
             nc.sync.dma_start(pos_sb[d][:], pos)
         nc.sync.dma_start(out=gates[:], in_=gate[:, 0:P, :].rearrange("d p v -> p d v"))
@@ -108,8 +100,8 @@ def tile_picked_sub_mlp_silu_sub_e_kernel(tc, xT, w1, w2, gate, offs, pos1, pos2
             )
 
         def cast_w1(g, engine, u, a0, a1):
-            src = w1_raw[g][:].rearrange("p j (a u e i) -> p u a j e i", u=2, i=2, e=2)[:, u, a0:a1]
-            dst = w1_grp[g][u][:].rearrange("p (e a i j) -> p a j e i", e=2, i=2, j=4)[:, a0:a1]
+            src = w1_raw[g][:].rearrange("p j (m u e) -> p u m j e", u=2, e=2)[:, u, 2 * a0 : 2 * a1]
+            dst = w1_grp[g][u][:].rearrange("p (e m j) -> p m j e", e=2, j=4)[:, 2 * a0 : 2 * a1]
             if engine == "v":
                 nc.vector.tensor_copy(dst, src)
             else:
@@ -172,11 +164,9 @@ def tile_picked_sub_mlp_silu_sub_e_kernel(tc, xT, w1, w2, gate, offs, pos1, pos2
                     layer1(acc_h[s][:, t, :], t, P * s, P * (s + 1), g, False, g == left[-1] and t == 0)
 
         def cast_w2(m):
-            b = m // (M_TILES - 1)
-            c0 = P * m - w2_cuts[b][0]
             nc.vector.tensor_copy(
                 w2_grp[m][:].rearrange("p (c i) j -> p c j i", i=4),
-                w2_raw[b][:, :, c0 : c0 + P].rearrange("p j (c i) -> p c j i", i=4),
+                w2_raw[:, :, P * m : P * (m + 1)].rearrange("p j (c i) -> p c j i", i=4),
             )
 
         def quant_w2(m):
@@ -185,15 +175,6 @@ def tile_picked_sub_mlp_silu_sub_e_kernel(tc, xT, w1, w2, gate, offs, pos1, pos2
                 scales=w2_bytes[m][:],
                 in_=w2_grp[m][:].rearrange("p c j -> p (c j)"),
             )
-
-        for m in range(M_TILES - 1):
-            cast_w2(m)
-        quant_w2(0)
-        quant_w2(1)
-        quant_w2(2)
-        h_words = sb("h_words", [P, S], U32, tag="w2_raw0")
-
-        acc_y0 = psum.tile([P, 2 * P], F32, name="acc_y0")
 
         def layer2(dst, m, c0, c1):
             nc.tensor.matmul_mx(
@@ -206,178 +187,171 @@ def tile_picked_sub_mlp_silu_sub_e_kernel(tc, xT, w1, w2, gate, offs, pos1, pos2
                 stop=True,
             )
 
-        def quant_h(grp, c0, c1):
+        def quant_h(s):
+            c0, c1 = h_cuts[s]
             nc.vector.quantize_mx(
                 out=h_words[:, c0:c1].bitcast(FP8X4),
                 scales=h_bytes[:, c0:c1],
-                in_=grp[:].rearrange("p n t -> p (n t)"),
+                in_=h_grp[s][:].rearrange("p n t -> p (n t)"),
             )
 
+        def bank(name, width, tag):
+            return psum.tile([P, width], F32, name=name, tag=tag)
+
+        def y_part(m, c0, c1, tag):
+            acc = bank(f"acc_y{m}_{c0}", c1 - c0, tag)
+            layer2(acc[:], m, c0, c1)
+            return acc
+
+        halves = V // P
+        acc_g = bank("acc_g", V, "acc_b1")
+        for u in range(halves):
+            nc.tensor.transpose(acc_g[:, P * u : P * (u + 1)], gate_rows[:, P * u : P * (u + 1)], ident[:])
+        gate_cols = sb("gate_cols", [P, halves, D], F32)
+        nc.scalar.activation(gate_cols[:], acc_g[:].rearrange("p (u c) -> p u c", u=halves)[:, :, 0:D], COPY)
+
+        for m in range(2):
+            cast_w2(m)
+        for m in range(2):
+            quant_w2(m)
+        cast_w2(2)
+        h_words = sb("h_words", [P, S], U32, tag="w2_grp0")
         for s, (c0, c1) in enumerate(h_cuts):
             for b0 in range(c0, c1, P):
                 b1 = min(b0 + P, c1)
                 src = acc_h[b0 // P][:, :, b0 % P : b0 % P + b1 - b0]
                 nc.scalar.activation(h_grp[s][:, b0 - c0 : b1 - c0, :], src.rearrange("p t n -> p n t"), SILU)
-        for s, (c0, c1) in enumerate(h_cuts):
-            quant_h(h_grp[s], c0, c1)
-            if s == 0:
-                layer2(acc_y0[:], 0, c0, c1)
-                acc_y1 = psum.tile([P, 2 * P], F32, name="acc_y1_early", tag="acc_h2")
-                layer2(acc_y1[:], 1, c0, c1)
-                acc_y2 = psum.tile([P, S], F32, name="acc_y2", tag="acc_b2")
-                layer2(acc_y2[:, c0:c1], 2, c0, c1)
-        cast_w2(M_TILES - 1)
-        quant_w2(3)
-        y_sb[1] = sb("y_sb1", [P, S], F32, tag=f"h_grp{len(h_cuts) - 1}")
-        nc.vector.tensor_copy(y_sb[1][:, : 2 * P], acc_y1[:])
-        nc.scalar.activation(y_sb[0][:, : 2 * P], acc_y0[:], COPY)
-        for (c0, c1), tag in zip(h_cuts[1:], ("acc_h0", "acc_b0", "acc_h1")):
-            acc_late = psum.tile([P, c1 - c0], F32, name=f"acc_late{c0}", tag=tag)
-            layer2(acc_late[:], 0, c0, c1)
-            nc.scalar.activation(y_sb[0][:, c0:c1], acc_late[:], COPY)
-        y_from = {1: 2 * P, 2: 0, 3: 0}
-        acc_y = {m: psum.tile([P, S - y_from[m]], F32, name=f"acc_y{m}", tag=tag) for m, tag in ((1, "acc_b1"), (3, "acc_h1"))}
-        acc_y[2] = acc_y2
-        layer2(acc_y[1][:], 1, 2 * P, S)
-        layer2(acc_y[2][:, 2 * P :], 2, 2 * P, S)
-        layer2(acc_y[3][:], 3, 0, S)
+        first = 2 * P
+        quant_h(0)
+        cast_w2(3)
+        early = {m: y_part(m, 0, first, tag)[:] for m, tag in ((0, "acc_y0"), (1, "acc_b2"))}
+        for s in range(1, len(h_cuts)):
+            quant_h(s)
+        for m in (2, 3):
+            quant_w2(m)
+        y_sb = {m: sb(f"y_sb{m}", [P, S], F32, tag="h_grp2" if m == 1 else None) for m in range(M_TILES)}
+        nc.vector.tensor_copy(y_sb[1][:, 0:first], early[1])
+        nc.scalar.activation(y_sb[0][:, 0:first], early[0], COPY)
+        for (c0, c1), tag in zip(h_cuts[1:], ("acc_h0", "acc_b1", "acc_h1")):
+            nc.scalar.activation(y_sb[0][:, c0:c1], y_part(0, c0, c1, tag)[:], COPY)
+        y_from = {1: first, 2: 0, 3: 0}
+        late = {m: y_part(m, y_from[m], S, tag) for m, tag in ((1, "acc_b0"), (2, "acc_h2"), (3, "acc_h3"))}
 
-        halves = V // P
-        last_tile = M_TILES - 1
-        sum_tags = {(0, 0): "acc_h2", (1, 0): "acc_h3", (2, 0): "acc_y0", (3, 0): "acc_h2", (3, 1): "acc_h3"}
-        back_tags = {(0, 0): "acc_b0", (1, 0): "acc_b1", (2, 0): "acc_b0", (3, 0): "acc_h0", (3, 1): "acc_b2"}
-        pick_tags = ("acc_h3", "acc_h0", "acc_b2", "acc_h1")
-        acc_p = {}
-        acc_t = {}
-        acc_o = {}
-        scaled = [sb(f"scaled{d}", [P, V], F32) for d in range(D)]
-        slot = {(m, d): terms[m][:, d, :] for m in range(M_TILES) for d in range(D)}
-        first = sb("first", [P, 3 * P], F32)
-        gate_cols = first[:, 0 : halves * D].rearrange("p (u d) -> p u d", d=D)
-        slot[0, 0] = first[:, 0:V]
-        slot[1, 0] = first[:, P : P + V]
-        slot[1, 1] = slot[0, 1]
-        slot[1, 2] = slot[0, 2]
-        slot[1, 3] = slot[2, 0]
-        slot[3, 0] = slot[1, 0]
-        slot[3, 1] = slot[1, 1]
-        slot[3, 2] = turned[0][:]
-        slot[2, 3] = scaled[0][:]
-        slot[3, 3] = slot[1, 3]
-        turns = {(m, u): 0 for m in range(M_TILES) for u in range(halves)}
-        through = (D, D, D - 1, D - 1)
+        def buf(name):
+            return sb(name, [P, V], F32)
 
-        def region(banks, tags, kind, m, u):
-            key = (m, u if m == last_tile else 0)
-            if key not in banks:
-                banks[key] = psum.tile([P, P if m == last_tile else V], F32, name=f"{kind}{m}_{key[1]}", tag=tags[key])
-            return banks[key][:] if m == last_tile else banks[key][:, P * u : P * (u + 1)]
+        def half(ap, u):
+            return ap[:, P * u : P * (u + 1)]
 
         def leave(m):
-            nc.scalar.activation(y_sb[m][:, y_from[m] :], acc_y[m][:], COPY)
+            nc.scalar.activation(y_sb[m][:, y_from[m] :], late[m][:], COPY)
 
-        def turn_and_add(m, d, u0=0, u1=halves):
-            for u in range(u0, u1):
-                first = turns[m, u] == 0 and (u == 0 or m == last_tile)
-                last = turns[m, u] == through[m] - 1 and (u == halves - 1 or m == last_tile)
-                nc.tensor.matmul(
-                    region(acc_t, sum_tags, "acc_t", m, u),
-                    lhsT=slot[m, d][:, P * u : P * (u + 1)],
-                    rhs=ident[:],
-                    start=first,
-                    stop=last,
-                    is_transpose=True,
-                )
-                turns[m, u] = turns[m, u] + 1
+        def turn(dst, src, start, stop):
+            nc.tensor.matmul(dst, lhsT=src, rhs=ident[:], start=start, stop=stop, is_transpose=True)
 
-        def fetch(m, d, u0=0, u1=halves, turn=True):
+        def turn_into(acc, src, start, stop):
+            for u in range(halves):
+                turn(half(acc, u), half(src, u), start and u == 0, stop and u == halves - 1)
+
+        def fetch(dst, m, d, u0=0, u1=halves):
             nc.vector.tensor_tensor(
-                slot[m, d][:, P * u0 : P * u1],
+                dst[:, P * u0 : P * u1],
                 y_sb[m][:].indirect(pos_sb[d][:, 8 * u0 : 8 * u1]),
                 gates[:, d, P * u0 : P * u1],
                 MULT,
             )
-            if turn:
-                turn_and_add(m, d, u0, u1)
 
-        def keep_term(m):
-            fetch(m, D - 1, turn=False)
+        def pick(dst, m, d, tag):
+            nc.scalar.activation(dst[:], y_sb[m][:].indirect(pos_sb[d][:]), COPY)
+            acc = bank(f"acc_p{m}_{d}", V, tag)
+            turn_into(acc, dst, True, True)
+            return acc
 
-        def pick(m, d):
-            nc.scalar.activation(slot[m, d], y_sb[m][:].indirect(pos_sb[d][:]), COPY)
-            acc_p[d] = psum.tile([P, V], F32, name=f"acc_p{d}", tag=pick_tags[d])
+        def scale(dst, picked, d):
             for u in range(halves):
-                nc.tensor.transpose(acc_p[d][:, P * u : P * (u + 1)], slot[m, d][:, P * u : P * (u + 1)], ident[:])
+                nc.scalar.activation(half(dst, u), half(picked, u), COPY, scale=gate_cols[:, u, d : d + 1])
 
-        def scale_back(m, d):
-            for u in range(halves):
-                cols = slice(P * u, P * (u + 1))
-                nc.scalar.activation(scaled[d][:, cols], acc_p[d][:, cols], COPY, scale=gate_cols[:, u, d : d + 1])
-            for u in range(halves):
-                nc.tensor.matmul(
-                    region(acc_o, back_tags, "acc_o", m, u),
-                    lhsT=scaled[d][:, P * u : P * (u + 1)],
-                    rhs=ident[:],
-                    start=d == 0 and u == 0,
-                    stop=d == D - 1 and u == halves - 1,
-                    is_transpose=True,
-                )
+        def turn_back(dst, acc, tag, m):
+            nc.scalar.activation(dst[:], acc[:], COPY)
+            back = bank(f"acc_o{m}", V, tag)
+            turn_into(back, dst, True, True)
+            return back
 
-        def turn_back(m, u0=0, u1=halves):
-            src = acc_t[m, u0][:] if m == last_tile else acc_t[m, 0][:]
-            nc.scalar.activation(turned[m][:, P * u0 : P * u1], src, COPY)
-            for u in range(u0, u1):
-                nc.tensor.transpose(region(acc_o, back_tags, "acc_o", m, u), turned[m][:, P * u : P * (u + 1)], ident[:])
+        def store(src, m, u0=0, u1=halves):
+            nc.sync.dma_start(out=out[P * m : P * (m + 1), P * u0 : P * u1], in_=src[:, P * u0 : P * u1])
 
-        def turn_gate():
-            acc_g = psum.tile([P, halves, P], F32, name="acc_g", tag="acc_b1")
-            for u in range(halves):
-                nc.tensor.transpose(acc_g[:, u, :], gate_rows[:, P * u : P * (u + 1)], ident[:])
-            nc.scalar.activation(gate_cols, acc_g[:, :, 0:D], COPY)
+        def finish_copy(back, m, res):
+            nc.scalar.activation(res[:], back[:], COPY)
+            store(res, m)
 
-        def store(m, u0=0, u1=halves):
-            nc.sync.dma_start(out=out[P * m : P * (m + 1), P * u0 : P * u1], in_=sums[m][:, P * u0 : P * u1])
+        term = {(m, d): buf(f"term{m}_{d}") for m in range(2) for d in range(D) if (m, d) != (1, 3)}
+        scaled = [buf(f"scaled{d}") for d in range(D)]
+        turned = {m: buf(f"turned{m}") for m in (0, 2, 3)}
+        term[1, 3] = term[0, 1]
+        term[2, 0] = buf("term2_0")
+        term[2, 1] = term[1, 0]
+        term[2, 2] = term[1, 1]
+        term[3, 0] = term[1, 2]
+        term[3, 1] = scaled[0]
+        term[3, 2] = term[1, 3]
+        term[2, 3] = turned[0]
+        term[3, 3] = scaled[2]
 
-        def finish_copy(m):
-            nc.scalar.activation(sums[m][:], acc_o[m, 0][:], COPY)
-            store(m)
+        def fetch_and_turn(acc, m, d, last):
+            fetch(term[m, d], m, d)
+            turn_into(acc, term[m, d], d == 0, d == last)
 
-        def finish_add(m, u0=0, u1=halves):
-            cols = slice(P * u0, P * u1)
-            nc.vector.tensor_tensor(sums[m][:, cols], acc_o[m, u0][:], slot[m, D - 1][:, cols], ADD)
-            store(m, u0, u1)
+        def scale_back(acc, picked, d):
+            scale(scaled[d], picked, d)
+            turn_into(acc, scaled[d], d == 0, d == D - 1)
 
         leave(1)
-        fetch(0, 0)
+        sum0 = bank("sum0", V, "acc_h1")
+        fetch_and_turn(sum0, 0, 0, 3)
+        picked = [pick(term[1, 0], 1, 0, "acc_b1")]
+        fetch_and_turn(sum0, 0, 1, 3)
+        picked.append(pick(term[1, 1], 1, 1, "acc_b2"))
         leave(2)
-        fetch(0, 1)
+        fetch_and_turn(sum0, 0, 2, 3)
+        fetch_and_turn(sum0, 0, 3, 3)
+        picked.append(pick(term[1, 2], 1, 2, "acc_b0"))
         leave(3)
-        turn_gate()
-        fetch(0, 2)
-        pick(1, 0)
-        fetch(0, 3)
-        pick(1, 1)
-        fetch(2, 0)
-        pick(1, 2)
-        fetch(2, 1)
-        turn_back(0)
-        fetch(2, 2)
-        scale_back(1, 0)
-        fetch(3, 0)
-        pick(1, 3)
-        scale_back(1, 1)
-        fetch(3, 1)
-        fetch(3, 2, 0, 1)
-        fetch(3, 2, 1, 2)
-        scale_back(1, 2)
-        scale_back(1, 3)
-        finish_copy(0)
-        keep_term(2)
-        turn_back(2)
-        turn_back(3, 0, 1)
-        turn_back(3, 1, 2)
-        keep_term(3)
-        finish_copy(1)
-        finish_add(2)
-        finish_add(3, 0, 1)
-        finish_add(3, 1, 2)
+        sum2 = bank("sum2", V, "acc_h0")
+        fetch_and_turn(sum2, 2, 0, 2)
+        out1 = bank("out1", V, "acc_y0")
+        scale_back(out1, picked[0], 0)
+        fetch_and_turn(sum2, 2, 1, 2)
+        picked.append(pick(term[1, 3], 1, 3, "acc_h2"))
+        scale_back(out1, picked[1], 1)
+        fetch_and_turn(sum2, 2, 2, 2)
+        back0 = turn_back(turned[0], sum0, "acc_h1", 0)
+        scale_back(out1, picked[2], 2)
+        sum3 = [bank(f"sum3_{u}", P, tag) for u, tag in enumerate(("acc_h3", "acc_b1"))]
+        for d in range(2):
+            fetch(term[3, d], 3, d)
+            for u in range(halves):
+                turn(sum3[u][:], half(term[3, d], u), d == 0, False)
+            if d == 0:
+                scale_back(out1, picked[3], 3)
+                finish_copy(back0, 0, buf("res0"))
+                back2 = turn_back(turned[2], sum2, "acc_h0", 2)
+        finish_copy(out1, 1, buf("res1"))
+        back3 = []
+        for u in range(halves):
+            fetch(term[3, 2], 3, 2, u, u + 1)
+            turn(sum3[u][:], half(term[3, 2], u), False, True)
+        for u, tag in enumerate(("acc_b2", "acc_b0")):
+            nc.scalar.activation(half(turned[3], u), sum3[u][:], COPY)
+            back3.append(bank(f"back3_{u}", P, tag))
+            turn(back3[u][:], half(turned[3], u), True, True)
+
+        fetch(term[2, 3], 2, 3)
+        fetch(term[3, 3], 3, 3, 0, 1)
+        res2 = buf("res2")
+        nc.vector.tensor_tensor(res2[:], back2[:], term[2, 3][:], ADD)
+        store(res2, 2)
+        fetch(term[3, 3], 3, 3, 1, 2)
+        res3 = buf("res3")
+        for u in range(halves):
+            nc.vector.tensor_tensor(half(res3, u), back3[u][:], half(term[3, 3], u), ADD)
+            store(res3, 3, u, u + 1)

from contextlib import ExitStack

import concourse.mybir as mybir
from concourse.masks import make_identity

K, T, S, H, N, V, D = 1536, 1024, 512, 512, 512, 256, 4
FLOPS = 2 * K * H * S + 2 * H * N * S

F32 = mybir.dt.float32
BF16 = mybir.dt.bfloat16
U32 = mybir.dt.uint32
U16 = mybir.dt.uint16
U8 = mybir.dt.uint8
FP8X4 = mybir.dt.float8_e4m3fn_x4
COPY = mybir.ActivationFunctionType.Copy
SILU = mybir.ActivationFunctionType.Silu
MULT = mybir.AluOpType.mult
ADD = mybir.AluOpType.add

P = 128
G = K // 512
M_TILES = N // P
W1_SHARE = ((64, 64), (0, 64), (0, 48))


def tile_picked_sub_mlp_silu_sub_e_kernel(tc, xT, w1, w2, gate, offs, pos1, pos2, pos3, pos4, out):
    nc = tc.nc
    with ExitStack() as ctx:
        keep = ctx.enter_context(tc.tile_pool(name="keep", bufs=1))
        psum = ctx.enter_context(tc.psum_pool(name="psum", bufs=1))

        def sb(name, shape, dtype, tag=None):
            return keep.tile(shape, dtype, name=name, tag=tag or name, align_bytes=64)

        offs_sb = sb("offs_sb", [P, S // 16], U16)
        pos_sb = [sb(f"pos_sb{d}", [P, V // 16], U16) for d in range(D)]
        slices = S // P
        x_cuts = ((0, 2), (2, 4))
        x_raw = [[sb(f"x_raw{g}_{j0}", [P, j1 - j0, T], F32) for j0, j1 in x_cuts] for g in range(G)]
        x_pick = [sb(f"x_pick{g}", [P, 4, S - P], F32) for g in range(G)]
        x_grp = [sb(f"x_grp{g}", [P, S, 4], BF16) for g in range(G)]
        p_words = [sb(f"p_words{g}", [P, S], U32) for g in range(G)]
        p_bytes = [sb(f"p_bytes{g}", [P, S], U8) for g in range(G)]
        w1_raw = [sb(f"w1_raw{g}", [P, 4, H], F32) for g in range(G)]
        w1_grp = [[sb(f"w1_grp{g}_{u}", [P, 2 * H], BF16) for u in range(2)] for g in range(G)]
        w1_words = [sb(f"w1_words{g}", [P, H], U32) for g in range(G)]
        w1_bytes = [sb(f"w1_bytes{g}", [P, H], U8) for g in range(G)]
        w2_raw = sb("w2_raw", [P, 4, N], F32)
        w2_grp = [sb(f"w2_grp{m}", [P, P, 4], BF16) for m in range(M_TILES)]
        w2_words = [sb(f"w2_words{m}", [P, P], U32) for m in range(M_TILES)]
        w2_bytes = [sb(f"w2_bytes{m}", [P, P], U8) for m in range(M_TILES)]
        h_cuts = ((0, 256), (256, 384), (384, 448), (448, 512))
        h_grp = [sb(f"h_grp{s}", [P, c1 - c0, 4], BF16) for s, (c0, c1) in enumerate(h_cuts)]
        h_bytes = sb("h_bytes", [P, S], U8)
        gates = sb("gates", [P, D, V], F32)
        gate_rows = sb("gate_rows", [P, V], F32)
        ident = sb("ident", [P, P], F32)

        nc.gpsimd.memset(gate_rows[:], 0.0)
        for g in range(G):
            rows = xT[512 * g : 512 * (g + 1), :].rearrange("(p j) t -> p j t", j=4)
            for e, (j0, j1) in enumerate(x_cuts):
                nc.sync.dma_start(out=x_raw[g][e][:], in_=rows[:, j0:j1, :])
                if g == 0 and e == 0:
                    nc.sync.dma_start(offs_sb[:], offs)
                    nc.sync.dma_start(out=gate_rows[0:D, :], in_=gate[:, P, :])
        for g in range(G):
            nc.sync.dma_start(out=w1_raw[g][:], in_=w1[512 * g : 512 * (g + 1), :].rearrange("(p j) c -> p j c", j=4))
        nc.sync.dma_start(out=w2_raw[:], in_=w2.rearrange("(p j) c -> p j c", j=4))
        for d, pos in enumerate((pos1, pos2, pos3, pos4)):
            nc.sync.dma_start(pos_sb[d][:], pos)
        nc.sync.dma_start(out=gates[:], in_=gate[:, 0:P, :].rearrange("d p v -> p d v"))

        make_identity(nc, ident[:])
        warm = sb("warm", [P, 2], F32)
        nc.vector.memset(warm[:, 0:1], 0.0)
        nc.scalar.activation(warm[:, 1:2], warm[:, 0:1], SILU)

        def gather_x(engine, dst, g, j, c0, c1):
            e = [k for k, (j0, j1) in enumerate(x_cuts) if j0 <= j < j1][0]
            src = x_raw[g][e][:, j - x_cuts[e][0], :].indirect(offs_sb[:, c0 // 16 : c1 // 16])
            if engine == "v":
                nc.vector.tensor_copy(dst, src)
            else:
                nc.scalar.activation(dst, src, COPY)

        def weave(engine, dst, src):
            dst = dst.rearrange("p (c i) j -> p c j i", i=4)
            src = src.rearrange("p j (c i) -> p c j i", i=4)
            if engine == "v":
                nc.vector.tensor_copy(dst, src)
            else:
                nc.scalar.copy(dst, src)

        def quant_x(grp, g, c0, c1):
            nc.vector.quantize_mx(
                out=p_words[g][:, c0:c1].bitcast(FP8X4),
                scales=p_bytes[g][:, c0:c1],
                in_=grp[:].rearrange("p c j -> p (c j)"),
            )

        def cast_w1(g, engine, u, a0, a1):
            src = w1_raw[g][:].rearrange("p j (m u e) -> p u m j e", u=2, e=2)[:, u, 2 * a0 : 2 * a1]
            dst = w1_grp[g][u][:].rearrange("p (e m j) -> p m j e", e=2, j=4)[:, 2 * a0 : 2 * a1]
            if engine == "v":
                nc.vector.tensor_copy(dst, src)
            else:
                nc.scalar.copy(dst, src)

        def quant_w1(g, t0, t1):
            nc.vector.quantize_mx(
                out=w1_words[g][:, P * t0 : P * t1].bitcast(FP8X4),
                scales=w1_bytes[g][:, P * t0 : P * t1],
                in_=w1_grp[g][t0 // 2][:, H * (t0 % 2) : H * (t0 % 2 + t1 - t0)],
            )

        for g in range(G):
            for j in range(4):
                cut = 2 * P if j >= 2 else P
                gather_x("v", x_grp[g][:, 0:P, j], g, j, 0, P)
                if cut > P:
                    gather_x("v", x_pick[g][:, j, 0 : cut - P], g, j, P, cut)
                gather_x("s", x_pick[g][:, j, cut - P :], g, j, cut, S)
            weave("v", x_grp[g][:, P:, :], x_pick[g][:])
            if g < G - 1:
                quant_x(x_grp[g], g, 0, S)

        acc_h = [psum.tile([P, 4, P], F32, name=f"acc_h{s}") for s in range(slices)]

        def layer1(dst, t, c0, c1, g, start, stop):
            words = p_words[g][:, c0:c1]
            nc.tensor.matmul_mx(
                out=dst,
                lhsT=w1_words[g][:, P * t : P * (t + 1)].bitcast(FP8X4),
                lhsT_scale=w1_bytes[g][:, P * t : P * (t + 1)],
                rhs=words.bitcast(FP8X4),
                rhs_scale=p_bytes[g][:, c0:c1],
                start=start,
                stop=stop,
            )

        for g in range(G):
            for u in range(2):
                split = W1_SHARE[g][u]
                if split > 0:
                    cast_w1(g, "s", u, 0, split)
                if split < P // 2:
                    cast_w1(g, "v", u, split, P // 2)
            quant_w1(g, 0, 2)
            if g < G - 1:
                quant_w1(g, 2, 4)
            else:
                quant_w1(g, 2, 3)
                quant_w1(g, 3, 4)
            if g == 0:
                quant_x(x_grp[G - 1], G - 1, 0, S)
            for s in range((slices, slices - 1, 1)[g]):
                for t in range(4):
                    layer1(acc_h[s][:, t, :], t, P * s, P * (s + 1), g, g == 0 and t == 0, g == G - 1 and t == 3)
        for s in range(1, slices):
            left = (2,) if s < slices - 1 else (2, 1)
            for g in left:
                for t in (3, 2, 1, 0):
                    layer1(acc_h[s][:, t, :], t, P * s, P * (s + 1), g, False, g == left[-1] and t == 0)

        def cast_w2(m):
            nc.vector.tensor_copy(
                w2_grp[m][:].rearrange("p (c i) j -> p c j i", i=4),
                w2_raw[:, :, P * m : P * (m + 1)].rearrange("p j (c i) -> p c j i", i=4),
            )

        def quant_w2(m):
            nc.vector.quantize_mx(
                out=w2_words[m][:].bitcast(FP8X4),
                scales=w2_bytes[m][:],
                in_=w2_grp[m][:].rearrange("p c j -> p (c j)"),
            )

        def layer2(dst, m, c0, c1):
            nc.tensor.matmul_mx(
                out=dst,
                lhsT=w2_words[m][:].bitcast(FP8X4),
                lhsT_scale=w2_bytes[m][:],
                rhs=h_words[:, c0:c1].bitcast(FP8X4),
                rhs_scale=h_bytes[:, c0:c1],
                start=True,
                stop=True,
            )

        def quant_h(s):
            c0, c1 = h_cuts[s]
            nc.vector.quantize_mx(
                out=h_words[:, c0:c1].bitcast(FP8X4),
                scales=h_bytes[:, c0:c1],
                in_=h_grp[s][:].rearrange("p n t -> p (n t)"),
            )

        def bank(name, width, tag):
            return psum.tile([P, width], F32, name=name, tag=tag)

        def y_part(m, c0, c1, tag):
            acc = bank(f"acc_y{m}_{c0}", c1 - c0, tag)
            layer2(acc[:], m, c0, c1)
            return acc

        halves = V // P
        acc_g = bank("acc_g", V, "acc_b1")
        for u in range(halves):
            nc.tensor.transpose(acc_g[:, P * u : P * (u + 1)], gate_rows[:, P * u : P * (u + 1)], ident[:])
        gate_cols = sb("gate_cols", [P, halves, D], F32)
        nc.scalar.activation(gate_cols[:], acc_g[:].rearrange("p (u c) -> p u c", u=halves)[:, :, 0:D], COPY)

        for m in range(2):
            cast_w2(m)
        for m in range(2):
            quant_w2(m)
        cast_w2(2)
        h_words = sb("h_words", [P, S], U32, tag="w2_grp0")
        for s, (c0, c1) in enumerate(h_cuts):
            for b0 in range(c0, c1, P):
                b1 = min(b0 + P, c1)
                src = acc_h[b0 // P][:, :, b0 % P : b0 % P + b1 - b0]
                nc.scalar.activation(h_grp[s][:, b0 - c0 : b1 - c0, :], src.rearrange("p t n -> p n t"), SILU)
        first = 2 * P
        quant_h(0)
        cast_w2(3)
        early = {m: y_part(m, 0, first, tag)[:] for m, tag in ((0, "acc_y0"), (1, "acc_b2"))}
        for s in range(1, len(h_cuts)):
            quant_h(s)
        for m in (2, 3):
            quant_w2(m)
        y_sb = {m: sb(f"y_sb{m}", [P, S], F32, tag="h_grp2" if m == 1 else None) for m in range(M_TILES)}
        nc.vector.tensor_copy(y_sb[1][:, 0:first], early[1])
        nc.scalar.activation(y_sb[0][:, 0:first], early[0], COPY)
        for (c0, c1), tag in zip(h_cuts[1:], ("acc_h0", "acc_b1", "acc_h1")):
            nc.scalar.activation(y_sb[0][:, c0:c1], y_part(0, c0, c1, tag)[:], COPY)
        y_from = {1: first, 2: 0, 3: 0}
        late = {m: y_part(m, y_from[m], S, tag) for m, tag in ((1, "acc_b0"), (2, "acc_h2"), (3, "acc_h3"))}

        def buf(name):
            return sb(name, [P, V], F32)

        def half(ap, u):
            return ap[:, P * u : P * (u + 1)]

        def leave(m):
            nc.scalar.activation(y_sb[m][:, y_from[m] :], late[m][:], COPY)

        def turn(dst, src, start, stop):
            nc.tensor.matmul(dst, lhsT=src, rhs=ident[:], start=start, stop=stop, is_transpose=True)

        def turn_into(acc, src, start, stop):
            for u in range(halves):
                turn(half(acc, u), half(src, u), start and u == 0, stop and u == halves - 1)

        def fetch(dst, m, d, u0=0, u1=halves):
            nc.vector.tensor_tensor(
                dst[:, P * u0 : P * u1],
                y_sb[m][:].indirect(pos_sb[d][:, 8 * u0 : 8 * u1]),
                gates[:, d, P * u0 : P * u1],
                MULT,
            )

        def pick(dst, m, d, tag):
            nc.scalar.activation(dst[:], y_sb[m][:].indirect(pos_sb[d][:]), COPY)
            acc = bank(f"acc_p{m}_{d}", V, tag)
            turn_into(acc, dst, True, True)
            return acc

        def scale(dst, picked, d):
            for u in range(halves):
                nc.scalar.activation(half(dst, u), half(picked, u), COPY, scale=gate_cols[:, u, d : d + 1])

        def turn_back(dst, acc, tag, m):
            nc.scalar.activation(dst[:], acc[:], COPY)
            back = bank(f"acc_o{m}", V, tag)
            turn_into(back, dst, True, True)
            return back

        def store(src, m, u0=0, u1=halves):
            nc.sync.dma_start(out=out[P * m : P * (m + 1), P * u0 : P * u1], in_=src[:, P * u0 : P * u1])

        def finish_copy(back, m, res):
            nc.scalar.activation(res[:], back[:], COPY)
            store(res, m)

        term = {(m, d): buf(f"term{m}_{d}") for m in range(2) for d in range(D) if (m, d) != (1, 3)}
        scaled = [buf(f"scaled{d}") for d in range(D)]
        turned = {m: buf(f"turned{m}") for m in (0, 2, 3)}
        term[1, 3] = term[0, 1]
        term[2, 0] = buf("term2_0")
        term[2, 1] = term[1, 0]
        term[2, 2] = term[1, 1]
        term[3, 0] = term[1, 2]
        term[3, 1] = scaled[0]
        term[3, 2] = term[1, 3]
        term[2, 3] = turned[0]
        term[3, 3] = scaled[2]

        def fetch_and_turn(acc, m, d, last):
            fetch(term[m, d], m, d)
            turn_into(acc, term[m, d], d == 0, d == last)

        def scale_back(acc, picked, d):
            scale(scaled[d], picked, d)
            turn_into(acc, scaled[d], d == 0, d == D - 1)

        leave(1)
        sum0 = bank("sum0", V, "acc_h1")
        fetch_and_turn(sum0, 0, 0, 3)
        picked = [pick(term[1, 0], 1, 0, "acc_b1")]
        fetch_and_turn(sum0, 0, 1, 3)
        picked.append(pick(term[1, 1], 1, 1, "acc_b2"))
        leave(2)
        fetch_and_turn(sum0, 0, 2, 3)
        fetch_and_turn(sum0, 0, 3, 3)
        picked.append(pick(term[1, 2], 1, 2, "acc_b0"))
        leave(3)
        sum2 = bank("sum2", V, "acc_h0")
        fetch_and_turn(sum2, 2, 0, 2)
        out1 = bank("out1", V, "acc_y0")
        scale_back(out1, picked[0], 0)
        fetch_and_turn(sum2, 2, 1, 2)
        picked.append(pick(term[1, 3], 1, 3, "acc_h2"))
        scale_back(out1, picked[1], 1)
        fetch_and_turn(sum2, 2, 2, 2)
        back0 = turn_back(turned[0], sum0, "acc_h1", 0)
        scale_back(out1, picked[2], 2)
        sum3 = [bank(f"sum3_{u}", P, tag) for u, tag in enumerate(("acc_h3", "acc_b1"))]
        for d in range(2):
            fetch(term[3, d], 3, d)
            for u in range(halves):
                turn(sum3[u][:], half(term[3, d], u), d == 0, False)
            if d == 0:
                scale_back(out1, picked[3], 3)
                finish_copy(back0, 0, buf("res0"))
                back2 = turn_back(turned[2], sum2, "acc_h0", 2)
        finish_copy(out1, 1, buf("res1"))
        back3 = []
        for u in range(halves):
            fetch(term[3, 2], 3, 2, u, u + 1)
            turn(sum3[u][:], half(term[3, 2], u), False, True)
        for u, tag in enumerate(("acc_b2", "acc_b0")):
            nc.scalar.activation(half(turned[3], u), sum3[u][:], COPY)
            back3.append(bank(f"back3_{u}", P, tag))
            turn(back3[u][:], half(turned[3], u), True, True)

        fetch(term[2, 3], 2, 3)
        fetch(term[3, 3], 3, 3, 0, 1)
        res2 = buf("res2")
        nc.vector.tensor_tensor(res2[:], back2[:], term[2, 3][:], ADD)
        store(res2, 2)
        fetch(term[3, 3], 3, 3, 1, 2)
        res3 = buf("res3")
        for u in range(halves):
            nc.vector.tensor_tensor(half(res3, u), back3[u][:], half(term[3, 3], u), ADD)
            store(res3, 3, u, u + 1)
